import numpy as np
import ml_dtypes


def mxq(x, axis, fmt="e4m3"):
    dtype, down = {"e4m3": (ml_dtypes.float8_e4m3fn, 7), "e5m2": (ml_dtypes.float8_e5m2, 14)}[fmt]
    v = np.moveaxis(np.asarray(x, np.float32).astype(ml_dtypes.bfloat16).astype(np.float64), axis, -1)
    blocks = v.reshape(v.shape[:-1] + (-1, 32))
    amax = np.abs(blocks).max(-1, keepdims=True)
    byte = np.maximum(np.where(amax > 0, np.frexp(amax)[1] - 1 + 127, 0) - down, 1)
    scale = np.exp2(byte - 127.0)
    codes = (blocks / scale).astype(np.float32).astype(dtype).astype(np.float64)
    return np.moveaxis((codes * scale).reshape(v.shape), -1, axis)


WIDE = False


def mx_kscale(k):
    if not WIDE:
        return np.ones(k)
    levels = np.array([10, -10, 5, -5, 0])
    if k % 512:
        return np.exp2(np.random.permutation(np.resize(levels, k // 32))).repeat(32)
    a = np.empty((k // 512, 16))
    for p in range(k // 512):
        a[p, :8] = np.random.permutation(np.resize(levels, 8))
        for g in range(8):
            far = levels[np.abs(levels - a[p, g]) >= 10]
            a[p, g + 8] = far[np.random.randint(len(far))]
    return np.exp2(a.ravel()).repeat(32)


def f64(x):
    return np.asarray(x).astype(np.float64)


def striped(idx):
    return np.tile(np.asarray(idx).reshape(-1, 16).T, (8, 1)).astype(np.uint16)


def unstriped(offs):
    return offs[:16].T.reshape(-1).astype(np.int64)


E2M1 = np.array([0.0, 0.5, 1.0, 1.5, 2.0, 3.0, 4.0, 6.0, -0.0, -0.5, -1.0, -1.5, -2.0, -3.0, -4.0, -6.0])


def pack_weight(w, fmt):
    k, n = w.shape
    w = f64(np.asarray(w, np.float32).astype(ml_dtypes.bfloat16)).reshape(k // 32, 32, n)
    amax = np.abs(w).max(1)
    if fmt == "e4m3":
        byte = np.frexp(amax)[1] - 1 + 127 - 7
    else:
        mant, ex = np.frexp(amax / 6.0)
        byte = np.where(mant > 0.5, ex, ex - 1) + 127
    byte = np.clip(np.where(amax > 0, byte, 1), 1, 254)
    scaled = (w * np.exp2(127.0 - byte)[:, None, :]).reshape(k, n).astype(np.float32)
    by_word = np.ascontiguousarray(scaled.reshape(k // 512, 128, 4, n).transpose(0, 1, 3, 2))
    if fmt == "e4m3":
        words = by_word.astype(ml_dtypes.float8_e4m3fn).view(np.uint8)
    else:
        c = by_word.astype(ml_dtypes.float4_e2m1fn).view(np.uint8) & 0xF
        words = (c[..., 0::2] | (c[..., 1::2] << 4)).reshape(k // 512, 128, 2 * n)
    return np.ascontiguousarray(words), np.ascontiguousarray(byte.astype(np.uint8).reshape(k // 512, 16, n))


def unpack_weight(words, scales, fmt):
    g, _, n = scales.shape
    words = np.ascontiguousarray(words).reshape(g, 128, n, -1)
    if fmt == "e4m3":
        vals = words.view(ml_dtypes.float8_e4m3fn).astype(np.float64)
    else:
        nib = np.empty((g, 128, n, 4), np.uint8)
        nib[..., 0::2] = words & 0xF
        nib[..., 1::2] = words >> 4
        vals = E2M1[nib]
    vals = vals * np.repeat(np.exp2(scales.astype(np.float64) - 127.0), 8, axis=1)[..., None]
    return vals.transpose(0, 1, 3, 2).reshape(g * 512, n)


B, N, T, D, DV, NQ = 1, 1024, 4096, 1024, 256, 256
PAGE = 512
CAP = 2.0


def setup_inputs():
    n = np.random.standard_normal
    pages = np.random.permutation(T // PAGE)[:B * N // PAGE]
    idx = (pages[:, None] * PAGE + np.arange(PAGE)[None, :]).reshape(-1)
    s = mx_kscale(D)[:, None]
    u = np.ones(T)
    u[idx] = mx_kscale(B * N)
    r = np.random.uniform(0.5, 2.0, T)
    k = n((D, T)) / s
    v = n((DV, T)) / (u * r)
    kp = pack_weight(k, "e2m1")
    vp = pack_weight(v.T, "e4m3")
    return {
        "qT": (n((B, D, NQ)) * s * (1.00 / np.sqrt(D))).astype(np.float32),
        "k_words": np.ascontiguousarray(kp[0].reshape(D // 1024, 2, 128, T, 2).transpose(0, 2, 3, 1, 4)).reshape(D // 1024, 128, T, 4),
        "k_scales": kp[1],
        "v_words": vp[0],
        "v_scales": vp[1],
        "vs": np.tile(u * r, (128, 1)).astype(np.float32),
        "og": n((B, NQ, DV)).astype(np.float32),
        "offs": striped(idx),
        "voffs": striped((pages[:, None] * DV + np.arange(DV)[None, :]).reshape(-1)),
    }


def reference(qT, k_words, k_scales, v_words, v_scales, vs, og, offs, voffs):
    idx = unstriped(offs)
    k = unpack_weight(k_words.reshape(D // 1024, 128, T, 2, 2).transpose(0, 3, 1, 2, 4).reshape(D // 512, 128, 2 * T), k_scales, "e2m1")
    v = unpack_weight(v_words, v_scales, "e4m3")
    v = v.reshape(T // 512, 512, DV)[unstriped(voffs)[::DV] // DV].reshape(B, N, DV)
    pick = lambda x: x[:, idx].reshape(x.shape[0], B, N).transpose(1, 0, 2)
    q = f64(qT)
    score = mxq(q, 1, "e4m3").transpose(0, 2, 1) @ pick(k)
    score = CAP * np.tanh(score / CAP)
    m = score.max(-1, keepdims=True)
    p = np.exp(score - m)
    total = p.sum(-1, keepdims=True)
    w = p * pick(f64(vs))[:, :1, :]
    y = mxq(w, 2, "e4m3") @ v
    y = y / total
    y = y / (1.0 + np.exp(-f64(og)))
    return y

@@ -1,0 +1,240 @@
+from contextlib import ExitStack
+
+import concourse.mybir as mybir
+from concourse.masks import make_identity
+
+F32 = mybir.dt.float32
+BF16 = mybir.dt.bfloat16
+I32 = mybir.dt.int32
+U32 = mybir.dt.uint32
+U16 = mybir.dt.uint16
+U8 = mybir.dt.uint8
+FP8X4 = mybir.dt.float8_e4m3fn_x4
+FP4X4 = mybir.dt.float4_e2m1fn_x4
+ACT = mybir.ActivationFunctionType
+ALU = mybir.AluOpType
+AXIS = mybir.AxisListType
+
+P = 128
+PACK = 4
+N, T, D, DV, NQ = 1024, 4096, 1024, 256, 256
+PAGE = 512
+CAP = 2.0
+PAGES = N // PAGE
+POOL_PAGES = T // PAGE
+PASSES = D // PAGE
+QT = NQ // P
+FLOPS = 2 * NQ * N * (D + DV)
+BYTES = 4 * D * NQ + 4 * P * T + 2 * 16 * T + 4 * P * DV * POOL_PAGES + 16 * DV * POOL_PAGES + 4 * T + 8 * NQ * DV
+
+
+def tile_attend_pkv4_gate_cap_kernel(
+    tc, qT, k_words, k_scales, v_words, v_scales, vs, og, offs, voffs, out
+):
+    nc = tc.nc
+    with ExitStack() as ctx:
+        lists = ctx.enter_context(tc.tile_pool(name="lists", bufs=1))
+        sb = ctx.enter_context(tc.tile_pool(name="sb", bufs=1))
+        ps = ctx.enter_context(tc.psum_pool(name="ps", bufs=1))
+
+        def sbt(name, shape, dtype, tag=None):
+            return sb.tile(shape, dtype, name=name, tag=tag or name, align_bytes=64)
+
+        def bank(name, tag, shape):
+            return ps.tile(shape, F32, name=name, tag=tag)
+
+        offs_sb = lists.tile([P, N // 16], U16, name="offs_sb")
+        voffs_sb = lists.tile([P, PAGES * DV // 16], U16, name="voffs_sb")
+        nc.sync.dma_start(offs_sb[:], offs)
+        nc.sync.dma_start(voffs_sb[:], voffs)
+
+        ks_pool = sbt("ks_pool", [P, T], U8, tag="ks_then_v")
+        nc.vector.memset(ks_pool[:].bitcast(I32), 0)
+        ks_rows = k_scales.rearrange("o (q f) t -> f q o t", f=PACK)
+        for f in range(PACK):
+            nc.scalar.dma_start(ks_pool[:].bitcast(I32)[f:P:16, :], ks_rows[f].bitcast(I32))
+
+        kw_pool = sbt("kw_pool", [P, T], I32)
+        nc.sync.dma_start(kw_pool[:], k_words[0].rearrange("p t b -> p (t b)").bitcast(I32))
+        q_raw = sbt("q_raw", [P, PASSES, PACK, NQ], F32)
+        nc.sync.dma_start(q_raw[:], qT[0].rearrange("(o p j) w -> p o j w", o=PASSES, j=PACK))
+
+        ident = sbt("ident", [P, P], F32)
+        make_identity(nc, ident[:])
+        warm = sbt("warm", [P, 1], F32)
+        nc.scalar.activation(out=warm[:], in_=ident[:, 0:1], func=ACT.Exp)
+
+        vs_pool = sbt("vs_pool", [P, T], F32, tag="vs_then_og")
+        nc.vector.memset(vs_pool[:].bitcast(I32), 0)
+        nc.scalar.dma_start(vs_pool[0:1, :], vs[0:1, :])
+
+        ks_shift = sbt("ks_shift", [P, N], U8)
+        nc.vector.memset(ks_shift[:].bitcast(I32), 0)
+        vsc_pool = sbt("vsc_pool", [P, POOL_PAGES * DV], U8)
+        nc.vector.memset(vsc_pool[:].bitcast(I32), 0)
+        vsc_rows = v_scales.rearrange("u (q f) e -> q f u e", f=PACK)
+        for q in range(4):
+            nc.sync.dma_start(
+                vsc_pool[:].bitcast(I32)[32 * q:32 * q + PACK, :].rearrange("f (u e) -> f u e", u=POOL_PAGES),
+                vsc_rows[q].bitcast(I32),
+            )
+
+        ks_g = sbt("ks_g", [P, N], U8)
+        nc.vector.tensor_copy(ks_g[:], ks_pool[:].indirect(offs_sb[:]))
+        nc.scalar.dma_start(ks_shift[:].bitcast(I32)[0:P - 16, :], ks_g[:].bitcast(I32)[16:P, :])
+        ks_plane = [ks_g, ks_shift]
+
+        vw_pool = sbt("vw_pool", [P, POOL_PAGES * DV], I32, tag="ks_then_v")
+        nc.sync.dma_start(
+            vw_pool[:].rearrange("p (u e) -> p u e", u=POOL_PAGES),
+            v_words.rearrange("u p e b -> p u (e b)").bitcast(I32),
+        )
+
+        vs_g = sbt("vs_g", [P, N], F32)
+        nc.vector.tensor_copy(vs_g[:], vs_pool[:].indirect(offs_sb[:]))
+
+        vs_col = sbt("vs_col", [P, PAGES, PACK], F32)
+        for g in range(PAGES):
+            vs_t = bank("vs_t%d" % g, "t%d" % g, [P, PACK, P])
+            for r in range(PACK):
+                nc.tensor.transpose(vs_t[:, r, :], vs_g[:, g * PAGE + r:(g + 1) * PAGE:PACK], ident[:])
+            nc.scalar.copy(vs_col[:, g, :], vs_t[:, :, 0])
+
+        q_bf = [sbt("q_bf%d" % h, [P, PASSES, P * PACK], BF16) for h in range(QT)]
+        for h in range(QT):
+            for o in range(PASSES):
+                nc.scalar.copy(
+                    q_bf[h][:, o, :].rearrange("p (c i t) -> p c t i", i=4, t=PACK),
+                    q_raw[:, o, :, h * P:(h + 1) * P].rearrange("p t (c i) -> p c t i", i=4),
+                )
+        q_codes = [sbt("q_codes%d" % h, [P, PASSES * P], U32) for h in range(QT)]
+        q_scales = [sbt("q_scales%d" % h, [P, PASSES * P], U8) for h in range(QT)]
+
+        def quantize_q(h):
+            nc.vector.quantize_mx(
+                out=q_codes[h][:].bitcast(FP8X4), scales=q_scales[h][:],
+                in_=q_bf[h][:].rearrange("p o x -> p (o x)"),
+            )
+
+        k_parted = [None] * PAGES
+
+        def gather_keys(g):
+            k_g = sbt("k_g%d" % g, [P, PAGE], U32, tag=("vs_then_og", "kg_then_vsc")[g])
+            cols = slice(g * PAGE // 16, (g + 1) * PAGE // 16)
+            nc.vector.tensor_copy(k_g[:], kw_pool[:].bitcast(U32).indirect(offs_sb[:, cols]))
+            k_parted[g] = sbt("k_parted%d" % g, [P, PASSES * PAGE * 2], U8)
+            nc.vector.tensor_copy(
+                k_parted[g][:].bitcast(U16).rearrange("p (o n) -> p o n", o=PASSES),
+                k_g[:].bitcast(U16).rearrange("p (n o) -> p o n", o=PASSES),
+            )
+
+        half = [sbt("half%d" % h, [P, N], F32) for h in range(QT)]
+
+        acc = [[bank("score%d%d" % (h, g), "s%d" % (2 * h + g), [P, PAGE]) for g in range(PAGES)] for h in range(QT)]
+
+        def score_pass(o, h, g):
+            nc.tensor.matmul_mx(
+                out=acc[h][g][:],
+                lhsT=q_codes[h][:, o * P:(o + 1) * P].bitcast(FP8X4),
+                lhsT_scale=q_scales[h][:, o * P:(o + 1) * P],
+                rhs=k_parted[g][:, o * 2 * PAGE:(o + 1) * 2 * PAGE].bitcast(FP4X4),
+                rhs_scale=ks_plane[o][:, g * PAGE:(g + 1) * PAGE],
+                start=(o == 0), stop=(o == PASSES - 1),
+            )
+
+        def cap(h, g):
+            nc.scalar.activation(
+                out=half[h][:, g * PAGE:(g + 1) * PAGE].rearrange("p (r s) -> p r s", r=PACK),
+                in_=acc[h][g][:].rearrange("p (s r) -> p r s", r=PACK),
+                func=ACT.Tanh, scale=1.0 / CAP,
+            )
+
+        gather_keys(0)
+        og_sb = sbt("og_sb", [P, QT, DV], F32, tag="vs_then_og")
+        nc.sync.dma_start(og_sb[:], og[0].rearrange("(h p) e -> p h e", p=P))
+        quantize_q(0)
+        gather_keys(1)
+        quantize_q(1)
+        for h in range(QT):
+            for g in range(PAGES):
+                for o in range(PASSES):
+                    score_pass(o, h, g)
+                cap(h, g)
+
+        neg_c = [sbt("neg_c%d" % h, [P, N], F32) for h in range(QT)]
+        neg_m = [sbt("neg_m%d" % h, [P, 1], F32) for h in range(QT)]
+        prob = [[sbt("prob%d%d" % (h, g), [P, PAGE], F32) for g in range(PAGES)] for h in range(QT)]
+        part_sum = sbt("part_sum", [P, QT, PAGES], F32)
+
+        def softmax(h):
+            nc.vector.tensor_scalar(
+                out=neg_c[h][:], in0=half[h][:], scalar1=-CAP, scalar2=None,
+                op0=ALU.mult, op1=ALU.min, accum_out=neg_m[h][:],
+            )
+            for g in range(PAGES):
+                nc.scalar.activation(
+                    out=prob[h][g][:], in_=neg_c[h][:, g * PAGE:(g + 1) * PAGE], func=ACT.Exp,
+                    bias=neg_m[h][:], scale=-1.0, accum_out=part_sum[:, h, g:g + 1],
+                )
+
+        softmax(0)
+        softmax(1)
+        vsc_g = sbt("vsc_g", [P, PAGES * DV], U8, tag="kg_then_vsc")
+        nc.vector.tensor_copy(vsc_g[:], vsc_pool[:].indirect(voffs_sb[:]))
+        v_g = sbt("v_g", [P, PAGES * DV], U32)
+        nc.vector.tensor_copy(v_g[:], vw_pool[:].bitcast(U32).indirect(voffs_sb[:]))
+
+        gate_t = sbt("gate_t", [P, QT, DV], F32)
+        gate = sbt("gate", [P, QT, DV], F32)
+        nc.scalar.activation(out=gate_t[:], in_=og_sb[:], func=ACT.Tanh, scale=0.5)
+        nc.scalar.activation(out=gate[:], in_=gate_t[:], func=ACT.Copy, scale=0.5, bias=0.5)
+
+        w_bf = [[None] * PAGES for h in range(QT)]
+        w_codes = [[None] * PAGES for h in range(QT)]
+        w_scales = [[None] * PAGES for h in range(QT)]
+
+        def weigh(h, g):
+            p_t = bank("p_t%d%d" % (h, g), "t%d" % ((2 * h + g + 2) % 4), [P, PACK, P])
+            for r in range(PACK):
+                nc.tensor.transpose(p_t[:, r, :], prob[h][g][:, r * P:(r + 1) * P], ident[:])
+            w_bf[h][g] = sbt("w_bf%d%d" % (h, g), [P, P, PACK], BF16)
+            nc.vector.tensor_tensor(
+                out=w_bf[h][g][:], in0=p_t[:].rearrange("p r q -> p q r"),
+                in1=vs_col[:, g, :].unsqueeze(1).to_broadcast([P, P, PACK]), op=ALU.mult,
+            )
+
+        def quantize_w(h, g):
+            w_codes[h][g] = sbt("w_codes%d%d" % (h, g), [P, P], U32)
+            w_scales[h][g] = sbt("w_scales%d%d" % (h, g), [P, P], U8)
+            nc.vector.quantize_mx(
+                out=w_codes[h][g][:].bitcast(FP8X4), scales=w_scales[h][g][:],
+                in_=w_bf[h][g][:].rearrange("p q r -> p (q r)"),
+            )
+
+        y = [None] * QT
+        for h in range(QT):
+            for g in range(PAGES):
+                weigh(h, g)
+            for g in range(PAGES):
+                quantize_w(h, g)
+        for h in range(QT):
+            y[h] = bank("y%d" % h, "s%d" % h, [P, DV])
+            for g in range(PAGES):
+                nc.tensor.matmul_mx(
+                    out=y[h][:],
+                    lhsT=w_codes[h][g][:].bitcast(FP8X4), lhsT_scale=w_scales[h][g][:],
+                    rhs=v_g[:, g * DV:(g + 1) * DV].bitcast(FP8X4), rhs_scale=vsc_g[:, g * DV:(g + 1) * DV],
+                    start=(g == 0), stop=(g == PAGES - 1),
+                )
+
+        row_sum = sbt("row_sum", [P, QT], F32)
+        inv_sum = sbt("inv_sum", [P, QT], F32)
+        nc.vector.tensor_reduce(out=row_sum[:], in_=part_sum[:], axis=AXIS.X, op=ALU.add)
+        nc.vector.reciprocal(inv_sum[:], row_sum[:])
+        for h in range(QT):
+            res = sbt("res%d" % h, [P, DV], F32)
+            nc.vector.scalar_tensor_tensor(
+                out=res[:], in0=y[h][:], scalar=inv_sum[:, h:h + 1], in1=gate[:, h, :],
+                op0=ALU.mult, op1=ALU.mult,
+            )
+            nc.sync.dma_start(out[0, h * P:(h + 1) * P, :], res[:])

@@ -35,6 +35,8 @@ def tile_attend_pkv4_gate_cap_kernel(
     with ExitStack() as ctx:
         lists = ctx.enter_context(tc.tile_pool(name="lists", bufs=1))
         sb = ctx.enter_context(tc.tile_pool(name="sb", bufs=1))
+        big = ctx.enter_context(tc.tile_pool(name="big", bufs=1))
+        mid = ctx.enter_context(tc.tile_pool(name="mid", bufs=1))
         ps = ctx.enter_context(tc.psum_pool(name="ps", bufs=1))
 
         def sbt(name, shape, dtype, tag=None):
@@ -48,30 +50,49 @@ def tile_attend_pkv4_gate_cap_kernel(
         nc.sync.dma_start(offs_sb[:], offs)
         nc.sync.dma_start(voffs_sb[:], voffs)
 
-        ks_pool = sbt("ks_pool", [P, T], U8, tag="ks_then_v")
-        nc.vector.memset(ks_pool[:].bitcast(I32), 0)
+        def zero_shared(words, vector_share):
+            nc.gpsimd.memset(words[:, vector_share:], 0)
+            cut = vector_share // 2 - 1
+            nc.vector.memset(words[:, :cut], 0)
+            nc.vector.memset(words[:, cut:vector_share], 0)
+
+        warm_in = sbt("warm_in", [P, 1], F32)
+        nc.gpsimd.memset(warm_in[:], 0.0)
+        ks_pool = sbt("ks_pool", [P, T], U8)
+        zero_shared(ks_pool[:].bitcast(I32), 384)
         ks_rows = k_scales.rearrange("o (q f) t -> f q o t", f=PACK)
         for f in range(PACK):
-            nc.scalar.dma_start(ks_pool[:].bitcast(I32)[f:P:16, :], ks_rows[f].bitcast(I32))
+            nc.sync.dma_start(ks_pool[:].bitcast(I32)[f:P:16, :], ks_rows[f].bitcast(I32))
 
-        kw_pool = sbt("kw_pool", [P, T], I32)
+        og_sb = sbt("og_sb", [P, QT, DV], F32)
+        nc.sync.dma_start(og_sb[:], og[0].rearrange("(h p) e -> p h e", p=P))
+
+        warm = big.tile([P, PACK * NQ + 32], F32, name="warm", offset=4 * T - 64, align_bytes=64)
+        nc.scalar.activation(out=warm[:, 0:1], in_=warm_in[:], func=ACT.Exp)
+        kw_pool = big.tile([P, T], I32, name="kw_pool", offset=0, align_bytes=64)
         nc.sync.dma_start(kw_pool[:], k_words[0].rearrange("p t b -> p (t b)").bitcast(I32))
-        q_raw = sbt("q_raw", [P, PASSES, PACK, NQ], F32)
-        nc.sync.dma_start(q_raw[:], qT[0].rearrange("(o p j) w -> p o j w", o=PASSES, j=PACK))
+        q_raw = []
+        for o in range(PASSES):
+            q_raw.append(big.tile([P, PACK, NQ], F32, name="q_raw%d" % o, offset=4 * T + o * 4 * PACK * NQ, align_bytes=64))
+        for o in range(PASSES):
+            nc.sync.dma_start(q_raw[o][:], qT[0, o * PAGE:(o + 1) * PAGE, :].rearrange("(p j) w -> p j w", j=PACK))
 
-        ident = sbt("ident", [P, P], F32)
-        make_identity(nc, ident[:])
-        warm = sbt("warm", [P, 1], F32)
-        nc.scalar.activation(out=warm[:], in_=ident[:, 0:1], func=ACT.Exp)
-
-        vs_pool = sbt("vs_pool", [P, T], F32, tag="vs_then_og")
-        nc.vector.memset(vs_pool[:].bitcast(I32), 0)
+        vs_pool = mid.tile([P, T], F32, name="vs_pool", offset=0, align_bytes=64)
+        zero_shared(vs_pool[:].bitcast(I32), 1792)
         nc.scalar.dma_start(vs_pool[0:1, :], vs[0:1, :])
 
         ks_shift = sbt("ks_shift", [P, N], U8)
         nc.vector.memset(ks_shift[:].bitcast(I32), 0)
         vsc_pool = sbt("vsc_pool", [P, POOL_PAGES * DV], U8)
         nc.vector.memset(vsc_pool[:].bitcast(I32), 0)
+        ident = sbt("ident", [P, P], F32)
+        make_identity(nc, ident[:])
+
+        ks_g = sbt("ks_g", [P, N], U8)
+        nc.vector.tensor_copy(ks_g[:], ks_pool[:].indirect(offs_sb[:]))
+        nc.scalar.dma_start(ks_shift[:].bitcast(I32)[0:P - 16, :], ks_g[:].bitcast(I32)[16:P, :])
+        ks_plane = [ks_g, ks_shift]
+
         vsc_rows = v_scales.rearrange("u (q f) e -> q f u e", f=PACK)
         for q in range(4):
             nc.sync.dma_start(
@@ -79,34 +100,33 @@ def tile_attend_pkv4_gate_cap_kernel(
                 vsc_rows[q].bitcast(I32),
             )
 
-        ks_g = sbt("ks_g", [P, N], U8)
-        nc.vector.tensor_copy(ks_g[:], ks_pool[:].indirect(offs_sb[:]))
-        nc.scalar.dma_start(ks_shift[:].bitcast(I32)[0:P - 16, :], ks_g[:].bitcast(I32)[16:P, :])
-        ks_plane = [ks_g, ks_shift]
-
-        vw_pool = sbt("vw_pool", [P, POOL_PAGES * DV], I32, tag="ks_then_v")
+        vs_g = sbt("vs_g", [P, N], F32)
+        nc.vector.tensor_copy(vs_g[:], vs_pool[:].indirect(offs_sb[:]))
+        vw_pool = mid.tile([P, POOL_PAGES * DV], I32, name="vw_pool", offset=4 * N, align_bytes=64)
         nc.sync.dma_start(
             vw_pool[:].rearrange("p (u e) -> p u e", u=POOL_PAGES),
             v_words.rearrange("u p e b -> p u (e b)").bitcast(I32),
         )
 
-        vs_g = sbt("vs_g", [P, N], F32)
-        nc.vector.tensor_copy(vs_g[:], vs_pool[:].indirect(offs_sb[:]))
+        gate_t = sbt("gate_t", [P, QT, DV], F32)
+        gate = sbt("gate", [P, QT, DV], F32)
+        nc.scalar.activation(out=gate_t[:], in_=og_sb[:], func=ACT.Tanh, scale=0.5)
+        nc.scalar.activation(out=gate[:], in_=gate_t[:], func=ACT.Copy, scale=0.5, bias=0.5)
 
-        vs_col = sbt("vs_col", [P, PAGES, PACK], F32)
+        q_bf = [sbt("q_bf%d" % h, [P, PASSES, P * PACK], BF16) for h in range(QT)]
+        for o in range(PASSES):
+            for h in range(QT):
+                nc.scalar.copy(
+                    q_bf[h][:, o, :].rearrange("p (c i t) -> p c t i", i=4, t=PACK),
+                    q_raw[o][:, :, h * P:(h + 1) * P].rearrange("p t (c i) -> p c t i", i=4),
+                )
+        vs_col = big.tile([P, PAGES, PACK], F32, name="vs_col", offset=4 * T + 4 * PACK * NQ + 128, align_bytes=64)
         for g in range(PAGES):
             vs_t = bank("vs_t%d" % g, "t%d" % g, [P, PACK, P])
             for r in range(PACK):
                 nc.tensor.transpose(vs_t[:, r, :], vs_g[:, g * PAGE + r:(g + 1) * PAGE:PACK], ident[:])
             nc.scalar.copy(vs_col[:, g, :], vs_t[:, :, 0])
 
-        q_bf = [sbt("q_bf%d" % h, [P, PASSES, P * PACK], BF16) for h in range(QT)]
-        for h in range(QT):
-            for o in range(PASSES):
-                nc.scalar.copy(
-                    q_bf[h][:, o, :].rearrange("p (c i t) -> p c t i", i=4, t=PACK),
-                    q_raw[:, o, :, h * P:(h + 1) * P].rearrange("p t (c i) -> p c t i", i=4),
-                )
         q_codes = [sbt("q_codes%d" % h, [P, PASSES * P], U32) for h in range(QT)]
         q_scales = [sbt("q_scales%d" % h, [P, PASSES * P], U8) for h in range(QT)]
 
@@ -117,15 +137,16 @@ def tile_attend_pkv4_gate_cap_kernel(
             )
 
         k_parted = [None] * PAGES
+        k_g = mid.tile([P, N], U32, name="k_g", offset=0, align_bytes=64)
 
         def gather_keys(g):
-            k_g = sbt("k_g%d" % g, [P, PAGE], U32, tag=("vs_then_og", "kg_then_vsc")[g])
+            slots = slice(g * PAGE, (g + 1) * PAGE)
             cols = slice(g * PAGE // 16, (g + 1) * PAGE // 16)
-            nc.vector.tensor_copy(k_g[:], kw_pool[:].bitcast(U32).indirect(offs_sb[:, cols]))
+            nc.vector.tensor_copy(k_g[:, slots], kw_pool[:].bitcast(U32).indirect(offs_sb[:, cols]))
             k_parted[g] = sbt("k_parted%d" % g, [P, PASSES * PAGE * 2], U8)
             nc.vector.tensor_copy(
                 k_parted[g][:].bitcast(U16).rearrange("p (o n) -> p o n", o=PASSES),
-                k_g[:].bitcast(U16).rearrange("p (n o) -> p o n", o=PASSES),
+                k_g[:, slots].bitcast(U16).rearrange("p (n o) -> p o n", o=PASSES),
             )
 
         half = [sbt("half%d" % h, [P, N], F32) for h in range(QT)]
@@ -150,8 +171,6 @@ def tile_attend_pkv4_gate_cap_kernel(
             )
 
         gather_keys(0)
-        og_sb = sbt("og_sb", [P, QT, DV], F32, tag="vs_then_og")
-        nc.sync.dma_start(og_sb[:], og[0].rearrange("(h p) e -> p h e", p=P))
         quantize_q(0)
         gather_keys(1)
         quantize_q(1)
@@ -179,15 +198,10 @@ def tile_attend_pkv4_gate_cap_kernel(
 
         softmax(0)
         softmax(1)
-        vsc_g = sbt("vsc_g", [P, PAGES * DV], U8, tag="kg_then_vsc")
+        vsc_g = sbt("vsc_g", [P, PAGES * DV], U8, tag="q_bf0")
         nc.vector.tensor_copy(vsc_g[:], vsc_pool[:].indirect(voffs_sb[:]))
-        v_g = sbt("v_g", [P, PAGES * DV], U32)
+        v_g = sbt("v_g", [P, PAGES * DV], U32, tag="q_bf1")
         nc.vector.tensor_copy(v_g[:], vw_pool[:].bitcast(U32).indirect(voffs_sb[:]))
-
-        gate_t = sbt("gate_t", [P, QT, DV], F32)
-        gate = sbt("gate", [P, QT, DV], F32)
-        nc.scalar.activation(out=gate_t[:], in_=og_sb[:], func=ACT.Tanh, scale=0.5)
-        nc.scalar.activation(out=gate[:], in_=gate_t[:], func=ACT.Copy, scale=0.5, bias=0.5)
 
         w_bf = [[None] * PAGES for h in range(QT)]
         w_codes = [[None] * PAGES for h in range(QT)]

@@ -1,7 +1,6 @@
 from contextlib import ExitStack
 
 import concourse.mybir as mybir
-from concourse.masks import make_identity
 
 F32 = mybir.dt.float32
 BF16 = mybir.dt.bfloat16
@@ -58,46 +57,64 @@ def tile_attend_pkv4_gate_cap_kernel(
 
         warm_in = sbt("warm_in", [P, 1], F32)
         nc.gpsimd.memset(warm_in[:], 0.0)
+        warm = sbt("warm", [P, 1], F32)
+        nc.scalar.activation(out=warm[:], in_=warm_in[:], func=ACT.Exp)
+
+        vsc_pool = sbt("vsc_pool", [P, POOL_PAGES * DV], U8)
+        nc.gpsimd.memset(vsc_pool[:].bitcast(I32), 0)
+        nc.sync.dma_start(
+            vsc_pool[:].bitcast(I32)[0:16, :].rearrange("f (u e) -> f u e", u=POOL_PAGES),
+            v_scales.rearrange("u f e -> f u e").bitcast(I32),
+        )
+
         ks_pool = sbt("ks_pool", [P, T], U8)
-        zero_shared(ks_pool[:].bitcast(I32), 384)
+        zero_shared(ks_pool[:].bitcast(I32), 480)
         ks_rows = k_scales.rearrange("o (q f) t -> f q o t", f=PACK)
         for f in range(PACK):
             nc.sync.dma_start(ks_pool[:].bitcast(I32)[f:P:16, :], ks_rows[f].bitcast(I32))
 
-        og_sb = sbt("og_sb", [P, QT, DV], F32)
-        nc.sync.dma_start(og_sb[:], og[0].rearrange("(h p) e -> p h e", p=P))
+        q_raw = [None] * PASSES
+        q_rows = qT[0].rearrange("(o p j) w -> o p j w", o=PASSES, j=PACK)
+        q_raw[0] = sbt("q_raw0", [P, PACK, NQ], F32)
+        nc.sync.dma_start(q_raw[0][:], q_rows[0])
 
-        warm = big.tile([P, PACK * NQ + 32], F32, name="warm", offset=4 * T - 64, align_bytes=64)
-        nc.scalar.activation(out=warm[:, 0:1], in_=warm_in[:], func=ACT.Exp)
         kw_pool = big.tile([P, T], I32, name="kw_pool", offset=0, align_bytes=64)
-        nc.sync.dma_start(kw_pool[:], k_words[0].rearrange("p t b -> p (t b)").bitcast(I32))
-        q_raw = []
-        for o in range(PASSES):
-            q_raw.append(big.tile([P, PACK, NQ], F32, name="q_raw%d" % o, offset=4 * T + o * 4 * PACK * NQ, align_bytes=64))
-        for o in range(PASSES):
-            nc.sync.dma_start(q_raw[o][:], qT[0, o * PAGE:(o + 1) * PAGE, :].rearrange("(p j) w -> p j w", j=PACK))
+        kw_rows = k_words[0].rearrange("p t b -> p (t b)").bitcast(I32)
+        nc.sync.dma_start(kw_pool[:, 0:1536], kw_rows[:, 0:1536])
 
         vs_pool = mid.tile([P, T], F32, name="vs_pool", offset=0, align_bytes=64)
-        zero_shared(vs_pool[:].bitcast(I32), 1792)
-        nc.scalar.dma_start(vs_pool[0:1, :], vs[0:1, :])
+        zero_shared(vs_pool[:].bitcast(I32), 2048)
+        for c in range(2):
+            cols = slice(c * T // 2, (c + 1) * T // 2)
+            nc.sync.dma_start(vs_pool[0:1, cols], vs[0:1, cols])
 
-        ks_shift = sbt("ks_shift", [P, N], U8)
-        nc.vector.memset(ks_shift[:].bitcast(I32), 0)
-        vsc_pool = sbt("vsc_pool", [P, POOL_PAGES * DV], U8)
-        nc.vector.memset(vsc_pool[:].bitcast(I32), 0)
+        nc.sync.dma_start(kw_pool[:, 1536:2816], kw_rows[:, 1536:2816])
+        nc.sync.dma_start(kw_pool[:, 2816:T], kw_rows[:, 2816:T])
+        q_raw[1] = big.tile([P, PACK, NQ], F32, name="q_raw1", offset=4 * T, align_bytes=64)
+        nc.sync.dma_start(q_raw[1][:], q_rows[1])
+
+        zeros = sbt("zeros", [P, P], F32)
         ident = sbt("ident", [P, P], F32)
-        make_identity(nc, ident[:])
+        nc.gpsimd.memset(zeros[:], 0.0)
+        nc.gpsimd.affine_select(
+            out=ident[:], in_=zeros[:], pattern=[[-1, P]], compare_op=ALU.not_equal,
+            fill=1.0, base=0, channel_multiplier=1,
+        )
+        vsc_plane = sbt("vsc_plane", [P, PAGES * DV], U8)
+        nc.gpsimd.memset(vsc_plane[:].bitcast(I32), 0)
+        ks_shift = sbt("ks_shift", [P, N], U8)
+        nc.gpsimd.memset(ks_shift[:].bitcast(I32), 0)
 
+        vsc_g = sbt("vsc_g", [P, PAGES * DV], U8)
+        nc.vector.tensor_copy(vsc_g[:], vsc_pool[:].indirect(voffs_sb[:]))
         ks_g = sbt("ks_g", [P, N], U8)
         nc.vector.tensor_copy(ks_g[:], ks_pool[:].indirect(offs_sb[:]))
-        nc.scalar.dma_start(ks_shift[:].bitcast(I32)[0:P - 16, :], ks_g[:].bitcast(I32)[16:P, :])
+        nc.sync.dma_start(ks_shift[:].bitcast(I32)[0:P - 16, :], ks_g[:].bitcast(I32)[16:P, :])
         ks_plane = [ks_g, ks_shift]
-
-        vsc_rows = v_scales.rearrange("u (q f) e -> q f u e", f=PACK)
         for q in range(4):
             nc.sync.dma_start(
-                vsc_pool[:].bitcast(I32)[32 * q:32 * q + PACK, :].rearrange("f (u e) -> f u e", u=POOL_PAGES),
-                vsc_rows[q].bitcast(I32),
+                vsc_plane[:].bitcast(I32)[32 * q:32 * q + PACK, :],
+                vsc_g[:].bitcast(I32)[PACK * q:PACK * (q + 1), :],
             )
 
         vs_g = sbt("vs_g", [P, N], F32)
@@ -107,46 +124,43 @@ def tile_attend_pkv4_gate_cap_kernel(
             vw_pool[:].rearrange("p (u e) -> p u e", u=POOL_PAGES),
             v_words.rearrange("u p e b -> p u (e b)").bitcast(I32),
         )
+        og_sb = mid.tile([P, QT, DV], F32, name="og_sb", offset=4 * N + 4 * POOL_PAGES * DV, align_bytes=64)
+        nc.sync.dma_start(og_sb[:], og[0].rearrange("(h p) e -> p h e", p=P))
 
-        gate_t = sbt("gate_t", [P, QT, DV], F32)
-        gate = sbt("gate", [P, QT, DV], F32)
-        nc.scalar.activation(out=gate_t[:], in_=og_sb[:], func=ACT.Tanh, scale=0.5)
-        nc.scalar.activation(out=gate[:], in_=gate_t[:], func=ACT.Copy, scale=0.5, bias=0.5)
-
-        q_bf = [sbt("q_bf%d" % h, [P, PASSES, P * PACK], BF16) for h in range(QT)]
+        q_bf = [[None] * QT for o in range(PASSES)]
         for o in range(PASSES):
             for h in range(QT):
+                q_bf[o][h] = sbt("q_bf%d%d" % (o, h), [P, P * PACK], BF16)
                 nc.scalar.copy(
-                    q_bf[h][:, o, :].rearrange("p (c i t) -> p c t i", i=4, t=PACK),
+                    q_bf[o][h][:].rearrange("p (c i t) -> p c t i", i=4, t=PACK),
                     q_raw[o][:, :, h * P:(h + 1) * P].rearrange("p t (c i) -> p c t i", i=4),
                 )
-        vs_col = big.tile([P, PAGES, PACK], F32, name="vs_col", offset=4 * T + 4 * PACK * NQ + 128, align_bytes=64)
+        vs_col = big.tile([P, PAGES, PACK], F32, name="vs_col", offset=4 * T + 2048, align_bytes=64)
         for g in range(PAGES):
             vs_t = bank("vs_t%d" % g, "t%d" % g, [P, PACK, P])
             for r in range(PACK):
                 nc.tensor.transpose(vs_t[:, r, :], vs_g[:, g * PAGE + r:(g + 1) * PAGE:PACK], ident[:])
             nc.scalar.copy(vs_col[:, g, :], vs_t[:, :, 0])
 
-        q_codes = [sbt("q_codes%d" % h, [P, PASSES * P], U32) for h in range(QT)]
-        q_scales = [sbt("q_scales%d" % h, [P, PASSES * P], U8) for h in range(QT)]
+        q_codes = [[None] * QT for o in range(PASSES)]
+        q_scales = [[None] * QT for o in range(PASSES)]
 
-        def quantize_q(h):
+        def quantize_q(o, h):
+            q_codes[o][h] = sbt("q_codes%d%d" % (o, h), [P, P], U32)
+            q_scales[o][h] = sbt("q_scales%d%d" % (o, h), [P, P], U8)
             nc.vector.quantize_mx(
-                out=q_codes[h][:].bitcast(FP8X4), scales=q_scales[h][:],
-                in_=q_bf[h][:].rearrange("p o x -> p (o x)"),
+                out=q_codes[o][h][:].bitcast(FP8X4), scales=q_scales[o][h][:], in_=q_bf[o][h][:],
             )
 
         k_parted = [None] * PAGES
-        k_g = mid.tile([P, N], U32, name="k_g", offset=0, align_bytes=64)
 
-        def gather_keys(g):
-            slots = slice(g * PAGE, (g + 1) * PAGE)
+        def gather_keys(g, k_g):
             cols = slice(g * PAGE // 16, (g + 1) * PAGE // 16)
-            nc.vector.tensor_copy(k_g[:, slots], kw_pool[:].bitcast(U32).indirect(offs_sb[:, cols]))
+            nc.vector.tensor_copy(k_g[:], kw_pool[:].bitcast(U32).indirect(offs_sb[:, cols]))
             k_parted[g] = sbt("k_parted%d" % g, [P, PASSES * PAGE * 2], U8)
             nc.vector.tensor_copy(
                 k_parted[g][:].bitcast(U16).rearrange("p (o n) -> p o n", o=PASSES),
-                k_g[:, slots].bitcast(U16).rearrange("p (n o) -> p o n", o=PASSES),
+                k_g[:].bitcast(U16).rearrange("p (n o) -> p o n", o=PASSES),
             )
 
         half = [sbt("half%d" % h, [P, N], F32) for h in range(QT)]
@@ -156,8 +170,8 @@ def tile_attend_pkv4_gate_cap_kernel(
         def score_pass(o, h, g):
             nc.tensor.matmul_mx(
                 out=acc[h][g][:],
-                lhsT=q_codes[h][:, o * P:(o + 1) * P].bitcast(FP8X4),
-                lhsT_scale=q_scales[h][:, o * P:(o + 1) * P],
+                lhsT=q_codes[o][h][:].bitcast(FP8X4),
+                lhsT_scale=q_scales[o][h][:],
                 rhs=k_parted[g][:, o * 2 * PAGE:(o + 1) * 2 * PAGE].bitcast(FP4X4),
                 rhs_scale=ks_plane[o][:, g * PAGE:(g + 1) * PAGE],
                 start=(o == 0), stop=(o == PASSES - 1),
@@ -170,37 +184,49 @@ def tile_attend_pkv4_gate_cap_kernel(
                 func=ACT.Tanh, scale=1.0 / CAP,
             )
 
-        gather_keys(0)
-        quantize_q(0)
-        gather_keys(1)
-        quantize_q(1)
         for h in range(QT):
-            for g in range(PAGES):
-                for o in range(PASSES):
-                    score_pass(o, h, g)
-                cap(h, g)
+            quantize_q(0, h)
+        gather_keys(0, mid.tile([P, PAGE], U32, name="k_g0", offset=0, align_bytes=64))
+        for h in range(QT):
+            score_pass(0, h, 0)
+        quantize_q(1, 0)
+        score_pass(1, 0, 0)
+        cap(0, 0)
+        quantize_q(1, 1)
+        score_pass(1, 1, 0)
+        cap(1, 0)
+        gather_keys(1, sbt("k_g1", [P, PAGE], U32, tag="q_bf10"))
+        for h in range(QT):
+            for o in range(PASSES):
+                score_pass(o, h, 1)
+            cap(h, 1)
 
         neg_c = [sbt("neg_c%d" % h, [P, N], F32) for h in range(QT)]
         neg_m = [sbt("neg_m%d" % h, [P, 1], F32) for h in range(QT)]
+        neg_m_first = [sbt("neg_m_first%d" % h, [P, 1], F32) for h in range(QT)]
         prob = [[sbt("prob%d%d" % (h, g), [P, PAGE], F32) for g in range(PAGES)] for h in range(QT)]
         part_sum = sbt("part_sum", [P, QT, PAGES], F32)
 
-        def softmax(h):
+        def row_max(h, cols, start, result):
             nc.vector.tensor_scalar(
-                out=neg_c[h][:], in0=half[h][:], scalar1=-CAP, scalar2=None,
-                op0=ALU.mult, op1=ALU.min, accum_out=neg_m[h][:],
+                out=neg_c[h][:, cols], in0=half[h][:, cols], scalar1=-CAP, scalar2=start,
+                op0=ALU.mult, op1=ALU.min, accum_out=result,
             )
+
+        def exps(h):
             for g in range(PAGES):
                 nc.scalar.activation(
                     out=prob[h][g][:], in_=neg_c[h][:, g * PAGE:(g + 1) * PAGE], func=ACT.Exp,
                     bias=neg_m[h][:], scale=-1.0, accum_out=part_sum[:, h, g:g + 1],
                 )
 
-        softmax(0)
-        softmax(1)
-        vsc_g = sbt("vsc_g", [P, PAGES * DV], U8, tag="q_bf0")
-        nc.vector.tensor_copy(vsc_g[:], vsc_pool[:].indirect(voffs_sb[:]))
-        v_g = sbt("v_g", [P, PAGES * DV], U32, tag="q_bf1")
+        for h in range(QT):
+            row_max(h, slice(0, PAGE), None, neg_m_first[h][:])
+        for h in range(QT):
+            row_max(h, slice(PAGE, N), neg_m_first[h][:], neg_m[h][:])
+        for h in range(QT):
+            exps(h)
+        v_g = sbt("v_g", [P, PAGES * DV], U32)
         nc.vector.tensor_copy(v_g[:], vw_pool[:].bitcast(U32).indirect(voffs_sb[:]))
 
         w_bf = [[None] * PAGES for h in range(QT)]
@@ -225,6 +251,12 @@ def tile_attend_pkv4_gate_cap_kernel(
                 in_=w_bf[h][g][:].rearrange("p q r -> p (q r)"),
             )
 
+        gate_t = sbt("gate_t", [P, QT, DV], F32, tag="neg_c1")
+        gate = [sbt("gate%d" % h, [P, DV], F32) for h in range(QT)]
+        for h in range(QT):
+            nc.scalar.activation(out=gate_t[:, h, :], in_=og_sb[:, h, :], func=ACT.Tanh, scale=0.5)
+            nc.scalar.activation(out=gate[h][:], in_=gate_t[:, h, :], func=ACT.Copy, scale=0.5, bias=0.5)
+
         y = [None] * QT
         for h in range(QT):
             for g in range(PAGES):
@@ -237,7 +269,7 @@ def tile_attend_pkv4_gate_cap_kernel(
                 nc.tensor.matmul_mx(
                     out=y[h][:],
                     lhsT=w_codes[h][g][:].bitcast(FP8X4), lhsT_scale=w_scales[h][g][:],
-                    rhs=v_g[:, g * DV:(g + 1) * DV].bitcast(FP8X4), rhs_scale=vsc_g[:, g * DV:(g + 1) * DV],
+                    rhs=v_g[:, g * DV:(g + 1) * DV].bitcast(FP8X4), rhs_scale=vsc_plane[:, g * DV:(g + 1) * DV],
                     start=(g == 0), stop=(g == PAGES - 1),
                 )
 
@@ -248,7 +280,7 @@ def tile_attend_pkv4_gate_cap_kernel(
         for h in range(QT):
             res = sbt("res%d" % h, [P, DV], F32)
             nc.vector.scalar_tensor_tensor(
-                out=res[:], in0=y[h][:], scalar=inv_sum[:, h:h + 1], in1=gate[:, h, :],
+                out=res[:], in0=y[h][:], scalar=inv_sum[:, h:h + 1], in1=gate[h][:],
                 op0=ALU.mult, op1=ALU.mult,
             )
             nc.sync.dma_start(out[0, h * P:(h + 1) * P, :], res[:])

@@ -12,10 +12,10 @@ FP8X4 = mybir.dt.float8_e4m3fn_x4
 FP4X4 = mybir.dt.float4_e2m1fn_x4
 ACT = mybir.ActivationFunctionType
 ALU = mybir.AluOpType
-AXIS = mybir.AxisListType
 
 P = 128
 PACK = 4
+QUADS = 4
 N, T, D, DV, NQ = 1024, 4096, 1024, 256, 256
 PAGE = 512
 CAP = 2.0
@@ -23,6 +23,7 @@ PAGES = N // PAGE
 POOL_PAGES = T // PAGE
 PASSES = D // PAGE
 QT = NQ // P
+KIB = 1024
 FLOPS = 2 * NQ * N * (D + DV)
 BYTES = 4 * D * NQ + 4 * P * T + 2 * 16 * T + 4 * P * DV * POOL_PAGES + 16 * DV * POOL_PAGES + 4 * T + 8 * NQ * DV
 
@@ -34,66 +35,59 @@ def tile_attend_pkv4_gate_cap_kernel(
     with ExitStack() as ctx:
         lists = ctx.enter_context(tc.tile_pool(name="lists", bufs=1))
         sb = ctx.enter_context(tc.tile_pool(name="sb", bufs=1))
-        big = ctx.enter_context(tc.tile_pool(name="big", bufs=1))
-        mid = ctx.enter_context(tc.tile_pool(name="mid", bufs=1))
+        arena = ctx.enter_context(tc.tile_pool(name="arena", bufs=1))
         ps = ctx.enter_context(tc.psum_pool(name="ps", bufs=1))
 
-        def sbt(name, shape, dtype, tag=None):
-            return sb.tile(shape, dtype, name=name, tag=tag or name, align_bytes=64)
+        def sbt(name, shape, dtype):
+            return sb.tile(shape, dtype, name=name, align_bytes=64)
+
+        def placed(name, shape, dtype, kib):
+            return arena.tile(shape, dtype, name=name, offset=kib * KIB, align_bytes=64)
 
         def bank(name, tag, shape):
             return ps.tile(shape, F32, name=name, tag=tag)
 
+        def zero_odd(words):
+            cut = words.shape[1] // 2 - 1
+            nc.vector.memset(words[:, :cut], 0)
+            nc.vector.memset(words[:, cut:], 0)
+
         offs_sb = lists.tile([P, N // 16], U16, name="offs_sb")
         voffs_sb = lists.tile([P, PAGES * DV // 16], U16, name="voffs_sb")
-        nc.sync.dma_start(offs_sb[:], offs)
-        nc.sync.dma_start(voffs_sb[:], voffs)
 
-        def zero_shared(words, vector_share):
-            nc.gpsimd.memset(words[:, vector_share:], 0)
-            cut = vector_share // 2 - 1
-            nc.vector.memset(words[:, :cut], 0)
-            nc.vector.memset(words[:, cut:vector_share], 0)
+        ks_pool = sbt("ks_pool", [P, T], U8)
+        ks_words = ks_pool[:].bitcast(I32)
+        nc.sync.dma_start(offs_sb[:], offs)
+        nc.sync.dma_start(ks_words[0:32, :], k_scales.rearrange("o r t -> r o t").bitcast(I32))
+        vsc_pool = placed("vsc_pool", [P, POOL_PAGES * DV], U8, 10)
+        nc.gpsimd.memset(vsc_pool[:].bitcast(I32), 0)
+        nc.sync.dma_start(
+            vsc_pool[:].bitcast(I32)[0:16, :].rearrange("f (u e) -> f u e", u=POOL_PAGES),
+            v_scales.rearrange("u f e -> f u e").bitcast(I32),
+        )
+        nc.sync.dma_start(voffs_sb[:], voffs)
+        kw_pool = sbt("kw_pool", [P, T], I32)
+        nc.sync.dma_start(kw_pool[:], k_words[0].rearrange("p t b -> p (t b)").bitcast(I32))
+        q_rows = qT[0].rearrange("(o p j) w -> o p j w", o=PASSES, j=PACK)
+        q_raw = [placed("q_raw%d" % o, [P, PACK, NQ], F32, 4 * o) for o in range(PASSES)]
+        for o in range(PASSES):
+            nc.sync.dma_start(q_raw[o][:], q_rows[o])
 
         warm_in = sbt("warm_in", [P, 1], F32)
         nc.gpsimd.memset(warm_in[:], 0.0)
         warm = sbt("warm", [P, 1], F32)
         nc.scalar.activation(out=warm[:], in_=warm_in[:], func=ACT.Exp)
 
-        vsc_pool = sbt("vsc_pool", [P, POOL_PAGES * DV], U8)
-        nc.gpsimd.memset(vsc_pool[:].bitcast(I32), 0)
-        nc.sync.dma_start(
-            vsc_pool[:].bitcast(I32)[0:16, :].rearrange("f (u e) -> f u e", u=POOL_PAGES),
-            v_scales.rearrange("u f e -> f u e").bitcast(I32),
-        )
+        zero_odd(ks_words[32:64, :])
+        nc.gpsimd.memset(ks_words[64:P, :], 0)
+        ks_plane = sbt("ks_plane", [P, PASSES * N], U8)
+        zero_odd(ks_plane[:].bitcast(I32))
 
-        ks_pool = sbt("ks_pool", [P, T], U8)
-        zero_shared(ks_pool[:].bitcast(I32), 480)
-        ks_rows = k_scales.rearrange("o (q f) t -> f q o t", f=PACK)
-        for f in range(PACK):
-            nc.sync.dma_start(ks_pool[:].bitcast(I32)[f:P:16, :], ks_rows[f].bitcast(I32))
+        vs_pool = sbt("vs_pool", [P, T], F32)
+        for c in range(4):
+            nc.gpsimd.memset(vs_pool[:, c * T // 4:(c + 1) * T // 4], 0.0)
 
-        q_raw = [None] * PASSES
-        q_rows = qT[0].rearrange("(o p j) w -> o p j w", o=PASSES, j=PACK)
-        q_raw[0] = sbt("q_raw0", [P, PACK, NQ], F32)
-        nc.sync.dma_start(q_raw[0][:], q_rows[0])
-
-        kw_pool = big.tile([P, T], I32, name="kw_pool", offset=0, align_bytes=64)
-        kw_rows = k_words[0].rearrange("p t b -> p (t b)").bitcast(I32)
-        nc.sync.dma_start(kw_pool[:, 0:1536], kw_rows[:, 0:1536])
-
-        vs_pool = mid.tile([P, T], F32, name="vs_pool", offset=0, align_bytes=64)
-        zero_shared(vs_pool[:].bitcast(I32), 2048)
-        for c in range(2):
-            cols = slice(c * T // 2, (c + 1) * T // 2)
-            nc.sync.dma_start(vs_pool[0:1, cols], vs[0:1, cols])
-
-        nc.sync.dma_start(kw_pool[:, 1536:2816], kw_rows[:, 1536:2816])
-        nc.sync.dma_start(kw_pool[:, 2816:T], kw_rows[:, 2816:T])
-        q_raw[1] = big.tile([P, PACK, NQ], F32, name="q_raw1", offset=4 * T, align_bytes=64)
-        nc.sync.dma_start(q_raw[1][:], q_rows[1])
-
-        zeros = sbt("zeros", [P, P], F32)
+        zeros = placed("zeros", [P, P], F32, 12)
         ident = sbt("ident", [P, P], F32)
         nc.gpsimd.memset(zeros[:], 0.0)
         nc.gpsimd.affine_select(
@@ -102,185 +96,156 @@ def tile_attend_pkv4_gate_cap_kernel(
         )
         vsc_plane = sbt("vsc_plane", [P, PAGES * DV], U8)
         nc.gpsimd.memset(vsc_plane[:].bitcast(I32), 0)
-        ks_shift = sbt("ks_shift", [P, N], U8)
-        nc.gpsimd.memset(ks_shift[:].bitcast(I32), 0)
 
-        vsc_g = sbt("vsc_g", [P, PAGES * DV], U8)
-        nc.vector.tensor_copy(vsc_g[:], vsc_pool[:].indirect(voffs_sb[:]))
         ks_g = sbt("ks_g", [P, N], U8)
         nc.vector.tensor_copy(ks_g[:], ks_pool[:].indirect(offs_sb[:]))
-        nc.sync.dma_start(ks_shift[:].bitcast(I32)[0:P - 16, :], ks_g[:].bitcast(I32)[16:P, :])
-        ks_plane = [ks_g, ks_shift]
-        for q in range(4):
+        for q in range(QUADS):
+            nc.scalar.dma_start(
+                ks_plane[:].bitcast(I32)[32 * q:32 * q + PACK, :],
+                ks_g[:].bitcast(I32)[8 * q:8 * (q + 1), :],
+            )
+        nc.scalar.dma_start(vs_pool[0:1, :], vs[0:1, :])
+        vsc_g = sbt("vsc_g", [P, PAGES * DV], U8)
+        nc.vector.tensor_copy(vsc_g[:], vsc_pool[:].indirect(voffs_sb[:]))
+
+        og_sb = placed("og_sb", [P, QT, DV], F32, 10)
+        nc.sync.dma_start(og_sb[:], og[0].rearrange("(h p) e -> p h e", p=P))
+        vw_pool = placed("vw_pool", [P, POOL_PAGES * DV], I32, 12)
+        nc.sync.dma_start(
+            vw_pool[:].rearrange("p (u e) -> p u e", u=POOL_PAGES),
+            v_words.rearrange("u p e b -> p u (e b)").bitcast(I32),
+        )
+
+        k_g = [sbt("k_g%d" % g, [P, PAGE], U32) for g in range(PAGES)]
+        for g in range(PAGES):
+            cols = slice(g * PAGE // 16, (g + 1) * PAGE // 16)
+            nc.vector.tensor_copy(k_g[g][:], kw_pool[:].bitcast(U32).indirect(offs_sb[:, cols]))
+
+        q_bf = [sbt("q_bf%d" % h, [P, PASSES, P * PACK], BF16) for h in range(QT)]
+        for o in range(PASSES):
+            for h in range(QT):
+                nc.scalar.copy(
+                    q_bf[h][:, o, :].rearrange("p (c i t) -> p c t i", i=4, t=PACK),
+                    q_raw[o][:, :, h * P:(h + 1) * P].rearrange("p t (c i) -> p c t i", i=4),
+                )
+        q_codes = [sbt("q_codes%d" % h, [P, PASSES * P], U32) for h in range(QT)]
+        q_scales = [sbt("q_scales%d" % h, [P, PASSES * P], U8) for h in range(QT)]
+        k_parted = [sbt("k_parted0", [P, PASSES * PAGE * 2], U8), placed("k_parted1", [P, PASSES * PAGE * 2], U8, 4)]
+        for g in range(PAGES):
+            nc.vector.tensor_copy(
+                k_parted[g][:].bitcast(U16).rearrange("p (o n) -> p o n", o=PASSES),
+                k_g[g][:].bitcast(U16).rearrange("p (n o) -> p o n", o=PASSES),
+            )
+            h = g
+            nc.vector.quantize_mx(
+                out=q_codes[h][:].bitcast(FP8X4), scales=q_scales[h][:],
+                in_=q_bf[h][:].rearrange("p o c -> p (o c)"),
+            )
+
+        vs_g = placed("vs_g", [P, N], F32, 6)
+        nc.vector.tensor_copy(vs_g[:], vs_pool[:].indirect(offs_sb[:]))
+        vs_col = [sbt("vs_col%d" % g, [P, PACK], F32) for g in range(PAGES)]
+        for g in range(PAGES):
+            nc.sync.dma_start(vs_col[g][:], vs_g[0:1, g * PAGE:(g + 1) * PAGE])
+        for q in range(QUADS):
             nc.sync.dma_start(
                 vsc_plane[:].bitcast(I32)[32 * q:32 * q + PACK, :],
                 vsc_g[:].bitcast(I32)[PACK * q:PACK * (q + 1), :],
             )
 
-        vs_g = sbt("vs_g", [P, N], F32)
-        nc.vector.tensor_copy(vs_g[:], vs_pool[:].indirect(offs_sb[:]))
-        vw_pool = mid.tile([P, POOL_PAGES * DV], I32, name="vw_pool", offset=4 * N, align_bytes=64)
-        nc.sync.dma_start(
-            vw_pool[:].rearrange("p (u e) -> p u e", u=POOL_PAGES),
-            v_words.rearrange("u p e b -> p u (e b)").bitcast(I32),
-        )
-        og_sb = mid.tile([P, QT, DV], F32, name="og_sb", offset=4 * N + 4 * POOL_PAGES * DV, align_bytes=64)
-        nc.sync.dma_start(og_sb[:], og[0].rearrange("(h p) e -> p h e", p=P))
-
-        q_bf = [[None] * QT for o in range(PASSES)]
-        for o in range(PASSES):
-            for h in range(QT):
-                q_bf[o][h] = sbt("q_bf%d%d" % (o, h), [P, P * PACK], BF16)
-                nc.scalar.copy(
-                    q_bf[o][h][:].rearrange("p (c i t) -> p c t i", i=4, t=PACK),
-                    q_raw[o][:, :, h * P:(h + 1) * P].rearrange("p t (c i) -> p c t i", i=4),
-                )
-        vs_col = big.tile([P, PAGES, PACK], F32, name="vs_col", offset=4 * T + 2048, align_bytes=64)
-        for g in range(PAGES):
-            vs_t = bank("vs_t%d" % g, "t%d" % g, [P, PACK, P])
-            for r in range(PACK):
-                nc.tensor.transpose(vs_t[:, r, :], vs_g[:, g * PAGE + r:(g + 1) * PAGE:PACK], ident[:])
-            nc.scalar.copy(vs_col[:, g, :], vs_t[:, :, 0])
-
-        q_codes = [[None] * QT for o in range(PASSES)]
-        q_scales = [[None] * QT for o in range(PASSES)]
-
-        def quantize_q(o, h):
-            q_codes[o][h] = sbt("q_codes%d%d" % (o, h), [P, P], U32)
-            q_scales[o][h] = sbt("q_scales%d%d" % (o, h), [P, P], U8)
-            nc.vector.quantize_mx(
-                out=q_codes[o][h][:].bitcast(FP8X4), scales=q_scales[o][h][:], in_=q_bf[o][h][:],
-            )
-
-        k_parted = [None] * PAGES
-
-        def gather_keys(g, k_g):
-            cols = slice(g * PAGE // 16, (g + 1) * PAGE // 16)
-            nc.vector.tensor_copy(k_g[:], kw_pool[:].bitcast(U32).indirect(offs_sb[:, cols]))
-            k_parted[g] = sbt("k_parted%d" % g, [P, PASSES * PAGE * 2], U8)
-            nc.vector.tensor_copy(
-                k_parted[g][:].bitcast(U16).rearrange("p (o n) -> p o n", o=PASSES),
-                k_g[:].bitcast(U16).rearrange("p (n o) -> p o n", o=PASSES),
-            )
+        gate_t = sbt("gate_t", [P, QT, DV], F32)
+        gate = sbt("gate", [P, QT, DV], F32)
+        nc.scalar.activation(out=gate_t[:], in_=og_sb[:], func=ACT.Tanh, scale=0.5)
+        nc.scalar.activation(out=gate[:], in_=gate_t[:], func=ACT.Copy, scale=0.5, bias=0.5)
 
         half = [sbt("half%d" % h, [P, N], F32) for h in range(QT)]
-
         acc = [[bank("score%d%d" % (h, g), "s%d" % (2 * h + g), [P, PAGE]) for g in range(PAGES)] for h in range(QT)]
-
-        def score_pass(o, h, g):
-            nc.tensor.matmul_mx(
-                out=acc[h][g][:],
-                lhsT=q_codes[o][h][:].bitcast(FP8X4),
-                lhsT_scale=q_scales[o][h][:],
-                rhs=k_parted[g][:, o * 2 * PAGE:(o + 1) * 2 * PAGE].bitcast(FP4X4),
-                rhs_scale=ks_plane[o][:, g * PAGE:(g + 1) * PAGE],
-                start=(o == 0), stop=(o == PASSES - 1),
-            )
-
-        def cap(h, g):
-            nc.scalar.activation(
-                out=half[h][:, g * PAGE:(g + 1) * PAGE].rearrange("p (r s) -> p r s", r=PACK),
-                in_=acc[h][g][:].rearrange("p (s r) -> p r s", r=PACK),
-                func=ACT.Tanh, scale=1.0 / CAP,
-            )
-
         for h in range(QT):
-            quantize_q(0, h)
-        gather_keys(0, mid.tile([P, PAGE], U32, name="k_g0", offset=0, align_bytes=64))
-        for h in range(QT):
-            score_pass(0, h, 0)
-        quantize_q(1, 0)
-        score_pass(1, 0, 0)
-        cap(0, 0)
-        quantize_q(1, 1)
-        score_pass(1, 1, 0)
-        cap(1, 0)
-        gather_keys(1, sbt("k_g1", [P, PAGE], U32, tag="q_bf10"))
-        for h in range(QT):
-            for o in range(PASSES):
-                score_pass(o, h, 1)
-            cap(h, 1)
-
-        neg_c = [sbt("neg_c%d" % h, [P, N], F32) for h in range(QT)]
-        neg_m = [sbt("neg_m%d" % h, [P, 1], F32) for h in range(QT)]
-        neg_m_first = [sbt("neg_m_first%d" % h, [P, 1], F32) for h in range(QT)]
-        prob = [[sbt("prob%d%d" % (h, g), [P, PAGE], F32) for g in range(PAGES)] for h in range(QT)]
-        part_sum = sbt("part_sum", [P, QT, PAGES], F32)
-
-        def row_max(h, cols, start, result):
-            nc.vector.tensor_scalar(
-                out=neg_c[h][:, cols], in0=half[h][:, cols], scalar1=-CAP, scalar2=start,
-                op0=ALU.mult, op1=ALU.min, accum_out=result,
-            )
-
-        def exps(h):
             for g in range(PAGES):
+                for o in range(PASSES):
+                    nc.tensor.matmul_mx(
+                        out=acc[h][g][:],
+                        lhsT=q_codes[h][:, o * P:(o + 1) * P].bitcast(FP8X4),
+                        lhsT_scale=q_scales[h][:, o * P:(o + 1) * P],
+                        rhs=k_parted[g][:, o * 2 * PAGE:(o + 1) * 2 * PAGE].bitcast(FP4X4),
+                        rhs_scale=ks_plane[:, o * N + g * PAGE:o * N + (g + 1) * PAGE],
+                        start=(o == 0), stop=(o == PASSES - 1),
+                    )
                 nc.scalar.activation(
-                    out=prob[h][g][:], in_=neg_c[h][:, g * PAGE:(g + 1) * PAGE], func=ACT.Exp,
-                    bias=neg_m[h][:], scale=-1.0, accum_out=part_sum[:, h, g:g + 1],
+                    out=half[h][:, g * PAGE:(g + 1) * PAGE].rearrange("p (r s) -> p r s", r=PACK),
+                    in_=acc[h][g][:].rearrange("p (s r) -> p r s", r=PACK),
+                    func=ACT.Tanh, scale=1.0 / CAP,
                 )
 
+        neg_c = [placed("neg_c%d" % h, [P, N], F32, 20 + 4 * h) for h in range(QT)]
+        neg_m = [sbt("neg_m%d" % h, [P, 1], F32) for h in range(QT)]
+        prob = [sbt("prob%d" % h, [P, N], F32) for h in range(QT)]
+        row_sum = sbt("row_sum", [P, QT], F32)
         for h in range(QT):
-            row_max(h, slice(0, PAGE), None, neg_m_first[h][:])
+            nc.vector.tensor_scalar(
+                out=neg_c[h][:], in0=half[h][:], scalar1=-CAP, scalar2=None,
+                op0=ALU.mult, op1=ALU.min, accum_out=neg_m[h][:],
+            )
         for h in range(QT):
-            row_max(h, slice(PAGE, N), neg_m_first[h][:], neg_m[h][:])
-        for h in range(QT):
-            exps(h)
-        v_g = sbt("v_g", [P, PAGES * DV], U32)
+            nc.scalar.activation(
+                out=prob[h][:], in_=neg_c[h][:], func=ACT.Exp,
+                bias=neg_m[h][:], scale=-1.0, accum_out=row_sum[:, h:h + 1],
+            )
+        v_g = placed("v_g", [P, PAGES * DV], U32, 20)
         nc.vector.tensor_copy(v_g[:], vw_pool[:].bitcast(U32).indirect(voffs_sb[:]))
 
-        w_bf = [[None] * PAGES for h in range(QT)]
-        w_codes = [[None] * PAGES for h in range(QT)]
-        w_scales = [[None] * PAGES for h in range(QT)]
+        w_bf = [sbt("w_bf%d" % h, [P, PAGES, P, PACK], BF16) for h in range(QT)]
+        w_codes = [sbt("w_codes%d" % h, [P, PAGES * P], U32) for h in range(QT)]
+        w_scales = [sbt("w_scales%d" % h, [P, PAGES * P], U8) for h in range(QT)]
 
         def weigh(h, g):
-            p_t = bank("p_t%d%d" % (h, g), "t%d" % ((2 * h + g + 2) % 4), [P, PACK, P])
+            p_t = bank("p_t%d%d" % (h, g), "t%d" % (2 * h + g), [P, PACK, P])
             for r in range(PACK):
-                nc.tensor.transpose(p_t[:, r, :], prob[h][g][:, r * P:(r + 1) * P], ident[:])
-            w_bf[h][g] = sbt("w_bf%d%d" % (h, g), [P, P, PACK], BF16)
+                c = g * PAGE + r * P
+                nc.tensor.transpose(p_t[:, r, :], prob[h][:, c:c + P], ident[:])
             nc.vector.tensor_tensor(
-                out=w_bf[h][g][:], in0=p_t[:].rearrange("p r q -> p q r"),
-                in1=vs_col[:, g, :].unsqueeze(1).to_broadcast([P, P, PACK]), op=ALU.mult,
+                out=w_bf[h][:, g], in0=p_t[:].rearrange("p r q -> p q r"),
+                in1=vs_col[g][:].unsqueeze(1).to_broadcast([P, P, PACK]), op=ALU.mult,
             )
 
-        def quantize_w(h, g):
-            w_codes[h][g] = sbt("w_codes%d%d" % (h, g), [P, P], U32)
-            w_scales[h][g] = sbt("w_scales%d%d" % (h, g), [P, P], U8)
+        def quantize_w(h, pages):
+            cols = slice(pages.start * P, pages.stop * P)
             nc.vector.quantize_mx(
-                out=w_codes[h][g][:].bitcast(FP8X4), scales=w_scales[h][g][:],
-                in_=w_bf[h][g][:].rearrange("p q r -> p (q r)"),
+                out=w_codes[h][:, cols].bitcast(FP8X4), scales=w_scales[h][:, cols],
+                in_=w_bf[h][:, pages].rearrange("p g q r -> p (g q r)"),
             )
 
-        gate_t = sbt("gate_t", [P, QT, DV], F32, tag="neg_c1")
-        gate = [sbt("gate%d" % h, [P, DV], F32) for h in range(QT)]
-        for h in range(QT):
-            nc.scalar.activation(out=gate_t[:, h, :], in_=og_sb[:, h, :], func=ACT.Tanh, scale=0.5)
-            nc.scalar.activation(out=gate[h][:], in_=gate_t[:, h, :], func=ACT.Copy, scale=0.5, bias=0.5)
+        y = [bank("y%d" % h, "s%d" % h, [P, DV]) for h in range(QT)]
 
-        y = [None] * QT
-        for h in range(QT):
-            for g in range(PAGES):
-                weigh(h, g)
-            for g in range(PAGES):
-                quantize_w(h, g)
-        for h in range(QT):
-            y[h] = bank("y%d" % h, "s%d" % h, [P, DV])
-            for g in range(PAGES):
-                nc.tensor.matmul_mx(
-                    out=y[h][:],
-                    lhsT=w_codes[h][g][:].bitcast(FP8X4), lhsT_scale=w_scales[h][g][:],
-                    rhs=v_g[:, g * DV:(g + 1) * DV].bitcast(FP8X4), rhs_scale=vsc_plane[:, g * DV:(g + 1) * DV],
-                    start=(g == 0), stop=(g == PAGES - 1),
-                )
+        def value_pass(h, g):
+            nc.tensor.matmul_mx(
+                out=y[h][:],
+                lhsT=w_codes[h][:, g * P:(g + 1) * P].bitcast(FP8X4), lhsT_scale=w_scales[h][:, g * P:(g + 1) * P],
+                rhs=v_g[:, g * DV:(g + 1) * DV].bitcast(FP8X4), rhs_scale=vsc_plane[:, g * DV:(g + 1) * DV],
+                start=(g == 0), stop=(g == PAGES - 1),
+            )
 
-        row_sum = sbt("row_sum", [P, QT], F32)
         inv_sum = sbt("inv_sum", [P, QT], F32)
-        nc.vector.tensor_reduce(out=row_sum[:], in_=part_sum[:], axis=AXIS.X, op=ALU.add)
-        nc.vector.reciprocal(inv_sum[:], row_sum[:])
-        for h in range(QT):
+
+        def finish(h):
             res = sbt("res%d" % h, [P, DV], F32)
             nc.vector.scalar_tensor_tensor(
-                out=res[:], in0=y[h][:], scalar=inv_sum[:, h:h + 1], in1=gate[h][:],
+                out=res[:], in0=y[h][:], scalar=inv_sum[:, h:h + 1], in1=gate[:, h, :],
                 op0=ALU.mult, op1=ALU.mult,
             )
             nc.sync.dma_start(out[0, h * P:(h + 1) * P, :], res[:])
+
+        weigh(0, 0)
+        weigh(0, 1)
+        weigh(1, 0)
+        quantize_w(0, slice(0, PAGES))
+        weigh(1, 1)
+        value_pass(0, 0)
+        value_pass(0, 1)
+        quantize_w(1, slice(0, 1))
+        nc.vector.reciprocal(inv_sum[:], row_sum[:])
+        quantize_w(1, slice(1, PAGES))
+        value_pass(1, 0)
+        value_pass(1, 1)
+        finish(0)
+        finish(1)

@@ -24,6 +24,7 @@ POOL_PAGES = T // PAGE
 PASSES = D // PAGE
 QT = NQ // P
 KIB = 1024
+VS_VECTOR = 1024
 FLOPS = 2 * NQ * N * (D + DV)
 BYTES = 4 * D * NQ + 4 * P * T + 2 * 16 * T + 4 * P * DV * POOL_PAGES + 16 * DV * POOL_PAGES + 4 * T + 8 * NQ * DV
 
@@ -57,111 +58,112 @@ def tile_attend_pkv4_gate_cap_kernel(
 
         ks_pool = sbt("ks_pool", [P, T], U8)
         ks_words = ks_pool[:].bitcast(I32)
-        nc.sync.dma_start(offs_sb[:], offs)
-        nc.sync.dma_start(ks_words[0:32, :], k_scales.rearrange("o r t -> r o t").bitcast(I32))
-        vsc_pool = placed("vsc_pool", [P, POOL_PAGES * DV], U8, 10)
-        nc.gpsimd.memset(vsc_pool[:].bitcast(I32), 0)
-        nc.sync.dma_start(
-            vsc_pool[:].bitcast(I32)[0:16, :].rearrange("f (u e) -> f u e", u=POOL_PAGES),
-            v_scales.rearrange("u f e -> f u e").bitcast(I32),
-        )
-        nc.sync.dma_start(voffs_sb[:], voffs)
+        vs_pool = sbt("vs_pool", [P, T], F32)
         kw_pool = sbt("kw_pool", [P, T], I32)
+        nc.sync.dma_start(offs_sb[:], offs)
+        nc.sync.dma_start(ks_words[96:P, :], k_scales.rearrange("o r t -> r o t").bitcast(I32))
+        nc.sync.dma_start(vs_pool[P - 1:P, :], vs[0:1, :])
         nc.sync.dma_start(kw_pool[:], k_words[0].rearrange("p t b -> p (t b)").bitcast(I32))
-        q_rows = qT[0].rearrange("(o p j) w -> o p j w", o=PASSES, j=PACK)
-        q_raw = [placed("q_raw%d" % o, [P, PACK, NQ], F32, 4 * o) for o in range(PASSES)]
-        for o in range(PASSES):
-            nc.sync.dma_start(q_raw[o][:], q_rows[o])
 
         warm_in = sbt("warm_in", [P, 1], F32)
         nc.gpsimd.memset(warm_in[:], 0.0)
         warm = sbt("warm", [P, 1], F32)
         nc.scalar.activation(out=warm[:], in_=warm_in[:], func=ACT.Exp)
 
-        zero_odd(ks_words[32:64, :])
-        nc.gpsimd.memset(ks_words[64:P, :], 0)
+        zero_odd(ks_words[0:96, :])
+        zero_odd(vs_pool[0:P - 1, :VS_VECTOR])
+        nc.gpsimd.memset(vs_pool[0:P - 1, VS_VECTOR:], 0.0)
         ks_plane = sbt("ks_plane", [P, PASSES * N], U8)
-        zero_odd(ks_plane[:].bitcast(I32))
-
-        vs_pool = sbt("vs_pool", [P, T], F32)
-        for c in range(4):
-            nc.gpsimd.memset(vs_pool[:, c * T // 4:(c + 1) * T // 4], 0.0)
-
-        zeros = placed("zeros", [P, P], F32, 12)
-        ident = sbt("ident", [P, P], F32)
-        nc.gpsimd.memset(zeros[:], 0.0)
-        nc.gpsimd.affine_select(
-            out=ident[:], in_=zeros[:], pattern=[[-1, P]], compare_op=ALU.not_equal,
-            fill=1.0, base=0, channel_multiplier=1,
-        )
+        nc.gpsimd.memset(ks_plane[:].bitcast(I32), 0)
+        vsc_pool = sbt("vsc_pool", [P, POOL_PAGES * DV], U8)
+        nc.gpsimd.memset(vsc_pool[:].bitcast(I32)[0:112, :], 0)
         vsc_plane = sbt("vsc_plane", [P, PAGES * DV], U8)
         nc.gpsimd.memset(vsc_plane[:].bitcast(I32), 0)
+        ident = sbt("ident", [P, P], F32)
+        nc.gpsimd.memset(ident[:], 0.0)
+        nc.gpsimd.affine_select(
+            out=ident[:], in_=ident[:], pattern=[[-1, P]], compare_op=ALU.not_equal,
+            fill=1.0, base=0, channel_multiplier=1,
+        )
 
         ks_g = sbt("ks_g", [P, N], U8)
         nc.vector.tensor_copy(ks_g[:], ks_pool[:].indirect(offs_sb[:]))
         for q in range(QUADS):
-            nc.scalar.dma_start(
+            nc.sync.dma_start(
                 ks_plane[:].bitcast(I32)[32 * q:32 * q + PACK, :],
-                ks_g[:].bitcast(I32)[8 * q:8 * (q + 1), :],
+                ks_g[:].bitcast(I32)[96 + 8 * q:96 + 8 * (q + 1), :],
             )
-        nc.scalar.dma_start(vs_pool[0:1, :], vs[0:1, :])
-        vsc_g = sbt("vsc_g", [P, PAGES * DV], U8)
-        nc.vector.tensor_copy(vsc_g[:], vsc_pool[:].indirect(voffs_sb[:]))
+        vs_g = sbt("vs_g", [P, N], F32)
+        nc.vector.tensor_copy(vs_g[:], vs_pool[:].indirect(offs_sb[:]))
 
-        og_sb = placed("og_sb", [P, QT, DV], F32, 10)
-        nc.sync.dma_start(og_sb[:], og[0].rearrange("(h p) e -> p h e", p=P))
-        vw_pool = placed("vw_pool", [P, POOL_PAGES * DV], I32, 12)
+        q_rows = qT[0].rearrange("(o p j) w -> o p j w", o=PASSES, j=PACK)
+        q_raw = [[placed("q_raw%d%d" % (h, o), [P, PACK, P], F32, 4 * h + 2 * o) for o in range(PASSES)] for h in range(QT)]
+        for h in range(QT):
+            for o in range(PASSES):
+                nc.sync.dma_start(q_raw[h][o][:], q_rows[o][:, :, h * P:(h + 1) * P])
+        nc.sync.dma_start(
+            vsc_pool[:].bitcast(I32)[112:P, :].rearrange("f (u e) -> f u e", u=POOL_PAGES),
+            v_scales.rearrange("u f e -> f u e").bitcast(I32),
+        )
+        nc.sync.dma_start(voffs_sb[:], voffs)
+        vw_pool = sbt("vw_pool", [P, POOL_PAGES * DV], I32)
         nc.sync.dma_start(
             vw_pool[:].rearrange("p (u e) -> p u e", u=POOL_PAGES),
             v_words.rearrange("u p e b -> p u (e b)").bitcast(I32),
         )
-
-        k_g = [sbt("k_g%d" % g, [P, PAGE], U32) for g in range(PAGES)]
+        vs_col = [sbt("vs_col%d" % g, [P, PACK], F32) for g in range(PAGES)]
         for g in range(PAGES):
-            cols = slice(g * PAGE // 16, (g + 1) * PAGE // 16)
-            nc.vector.tensor_copy(k_g[g][:], kw_pool[:].bitcast(U32).indirect(offs_sb[:, cols]))
+            nc.sync.dma_start(vs_col[g][:], vs_g[P - 1:P, g * PAGE:(g + 1) * PAGE])
+        og_sb = sbt("og_sb", [P, QT, DV], F32)
+        nc.sync.dma_start(og_sb[:], og[0].rearrange("(h p) e -> p h e", p=P))
 
         q_bf = [sbt("q_bf%d" % h, [P, PASSES, P * PACK], BF16) for h in range(QT)]
-        for o in range(PASSES):
-            for h in range(QT):
+        for h in range(QT):
+            for o in range(PASSES):
                 nc.scalar.copy(
                     q_bf[h][:, o, :].rearrange("p (c i t) -> p c t i", i=4, t=PACK),
-                    q_raw[o][:, :, h * P:(h + 1) * P].rearrange("p t (c i) -> p c t i", i=4),
+                    q_raw[h][o][:].rearrange("p t (c i) -> p c t i", i=4),
                 )
         q_codes = [sbt("q_codes%d" % h, [P, PASSES * P], U32) for h in range(QT)]
         q_scales = [sbt("q_scales%d" % h, [P, PASSES * P], U8) for h in range(QT)]
-        k_parted = [sbt("k_parted0", [P, PASSES * PAGE * 2], U8), placed("k_parted1", [P, PASSES * PAGE * 2], U8, 4)]
-        for g in range(PAGES):
+        k_g = [sbt("k_g0", [P, PAGE], U32), placed("k_g1", [P, PAGE], U32, 2)]
+        k_parted = [sbt("k_parted0", [P, PASSES * PAGE * 2], U8), placed("k_parted1", [P, PASSES * PAGE * 2], U8, 6)]
+
+        def gather_keys(g):
+            cols = slice(g * PAGE // 16, (g + 1) * PAGE // 16)
+            nc.vector.tensor_copy(k_g[g][:], kw_pool[:].bitcast(U32).indirect(offs_sb[:, cols]))
+
+        def part_keys(g):
             nc.vector.tensor_copy(
                 k_parted[g][:].bitcast(U16).rearrange("p (o n) -> p o n", o=PASSES),
                 k_g[g][:].bitcast(U16).rearrange("p (n o) -> p o n", o=PASSES),
             )
-            h = g
+
+        def quantize_q(h):
             nc.vector.quantize_mx(
                 out=q_codes[h][:].bitcast(FP8X4), scales=q_scales[h][:],
                 in_=q_bf[h][:].rearrange("p o c -> p (o c)"),
             )
 
-        vs_g = placed("vs_g", [P, N], F32, 6)
-        nc.vector.tensor_copy(vs_g[:], vs_pool[:].indirect(offs_sb[:]))
-        vs_col = [sbt("vs_col%d" % g, [P, PACK], F32) for g in range(PAGES)]
-        for g in range(PAGES):
-            nc.sync.dma_start(vs_col[g][:], vs_g[0:1, g * PAGE:(g + 1) * PAGE])
+        gather_keys(0)
+        part_keys(0)
+        quantize_q(0)
+        gather_keys(1)
+        quantize_q(1)
+        part_keys(1)
+
+        vsc_g = sbt("vsc_g", [P, PAGES * DV], U8)
+        nc.vector.tensor_copy(vsc_g[:], vsc_pool[:].indirect(voffs_sb[:]))
         for q in range(QUADS):
             nc.sync.dma_start(
                 vsc_plane[:].bitcast(I32)[32 * q:32 * q + PACK, :],
-                vsc_g[:].bitcast(I32)[PACK * q:PACK * (q + 1), :],
+                vsc_g[:].bitcast(I32)[112 + PACK * q:112 + PACK * (q + 1), :],
             )
-
-        gate_t = sbt("gate_t", [P, QT, DV], F32)
-        gate = sbt("gate", [P, QT, DV], F32)
-        nc.scalar.activation(out=gate_t[:], in_=og_sb[:], func=ACT.Tanh, scale=0.5)
-        nc.scalar.activation(out=gate[:], in_=gate_t[:], func=ACT.Copy, scale=0.5, bias=0.5)
 
         half = [sbt("half%d" % h, [P, N], F32) for h in range(QT)]
         acc = [[bank("score%d%d" % (h, g), "s%d" % (2 * h + g), [P, PAGE]) for g in range(PAGES)] for h in range(QT)]
-        for h in range(QT):
-            for g in range(PAGES):
+        for g in range(PAGES):
+            for h in range(QT):
                 for o in range(PASSES):
                     nc.tensor.matmul_mx(
                         out=acc[h][g][:],
@@ -177,22 +179,32 @@ def tile_attend_pkv4_gate_cap_kernel(
                     func=ACT.Tanh, scale=1.0 / CAP,
                 )
 
-        neg_c = [placed("neg_c%d" % h, [P, N], F32, 20 + 4 * h) for h in range(QT)]
-        neg_m = [sbt("neg_m%d" % h, [P, 1], F32) for h in range(QT)]
-        prob = [sbt("prob%d" % h, [P, N], F32) for h in range(QT)]
+        neg_c = [[placed("neg_c%d%d" % (h, g), [P, PAGE], F32, 20 + 4 * h + 2 * g) for g in range(PAGES)] for h in range(QT)]
+        neg_m = [[sbt("neg_m%d%d" % (h, g), [P, 1], F32) for g in range(PAGES)] for h in range(QT)]
+        prob = [[sbt("prob%d%d" % (h, g), [P, PAGE], F32) for g in range(PAGES)] for h in range(QT)]
+        part_sum = sbt("part_sum", [P, PAGES, QT], F32)
         row_sum = sbt("row_sum", [P, QT], F32)
+        for g in range(PAGES):
+            for h in range(QT):
+                nc.vector.tensor_scalar(
+                    out=neg_c[h][g][:], in0=half[h][:, g * PAGE:(g + 1) * PAGE], scalar1=-CAP,
+                    scalar2=neg_m[h][0][:] if g else None,
+                    op0=ALU.mult, op1=ALU.min, accum_out=neg_m[h][g][:],
+                )
         for h in range(QT):
-            nc.vector.tensor_scalar(
-                out=neg_c[h][:], in0=half[h][:], scalar1=-CAP, scalar2=None,
-                op0=ALU.mult, op1=ALU.min, accum_out=neg_m[h][:],
-            )
-        for h in range(QT):
-            nc.scalar.activation(
-                out=prob[h][:], in_=neg_c[h][:], func=ACT.Exp,
-                bias=neg_m[h][:], scale=-1.0, accum_out=row_sum[:, h:h + 1],
-            )
+            for g in range(PAGES):
+                nc.scalar.activation(
+                    out=prob[h][g][:], in_=neg_c[h][g][:], func=ACT.Exp,
+                    bias=neg_m[h][PAGES - 1][:], scale=-1.0, accum_out=part_sum[:, g, h:h + 1],
+                )
+        nc.gpsimd.tensor_tensor(out=row_sum[:], in0=part_sum[:, 0, :], in1=part_sum[:, 1, :], op=ALU.add)
         v_g = placed("v_g", [P, PAGES * DV], U32, 20)
         nc.vector.tensor_copy(v_g[:], vw_pool[:].bitcast(U32).indirect(voffs_sb[:]))
+
+        gate_t = placed("gate_t", [P, QT, DV], F32, 26)
+        gate = sbt("gate", [P, QT, DV], F32)
+        nc.scalar.activation(out=gate_t[:], in_=og_sb[:], func=ACT.Tanh, scale=0.5)
+        nc.scalar.activation(out=gate[:], in_=gate_t[:], func=ACT.Copy, scale=0.5, bias=0.5)
 
         w_bf = [sbt("w_bf%d" % h, [P, PAGES, P, PACK], BF16) for h in range(QT)]
         w_codes = [sbt("w_codes%d" % h, [P, PAGES * P], U32) for h in range(QT)]
@@ -201,8 +213,7 @@ def tile_attend_pkv4_gate_cap_kernel(
         def weigh(h, g):
             p_t = bank("p_t%d%d" % (h, g), "t%d" % (2 * h + g), [P, PACK, P])
             for r in range(PACK):
-                c = g * PAGE + r * P
-                nc.tensor.transpose(p_t[:, r, :], prob[h][:, c:c + P], ident[:])
+                nc.tensor.transpose(p_t[:, r, :], prob[h][g][:, r * P:(r + 1) * P], ident[:])
             nc.vector.tensor_tensor(
                 out=w_bf[h][:, g], in0=p_t[:].rearrange("p r q -> p q r"),
                 in1=vs_col[g][:].unsqueeze(1).to_broadcast([P, P, PACK]), op=ALU.mult,

@@ -65,11 +65,6 @@ def tile_attend_pkv4_gate_cap_kernel(
         nc.sync.dma_start(vs_pool[P - 1:P, :], vs[0:1, :])
         nc.sync.dma_start(kw_pool[:], k_words[0].rearrange("p t b -> p (t b)").bitcast(I32))
 
-        warm_in = sbt("warm_in", [P, 1], F32)
-        nc.gpsimd.memset(warm_in[:], 0.0)
-        warm = sbt("warm", [P, 1], F32)
-        nc.scalar.activation(out=warm[:], in_=warm_in[:], func=ACT.Exp)
-
         zero_odd(ks_words[0:96, :])
         zero_odd(vs_pool[0:P - 1, :VS_VECTOR])
         nc.gpsimd.memset(vs_pool[0:P - 1, VS_VECTOR:], 0.0)
@@ -120,14 +115,14 @@ def tile_attend_pkv4_gate_cap_kernel(
         q_bf = [sbt("q_bf%d" % h, [P, PASSES, P * PACK], BF16) for h in range(QT)]
         for h in range(QT):
             for o in range(PASSES):
-                nc.scalar.copy(
-                    q_bf[h][:, o, :].rearrange("p (c i t) -> p c t i", i=4, t=PACK),
-                    q_raw[h][o][:].rearrange("p t (c i) -> p c t i", i=4),
+                nc.scalar.activation(
+                    out=q_bf[h][:, o, :].rearrange("p (c i t) -> p c t i", i=4, t=PACK),
+                    in_=q_raw[h][o][:].rearrange("p t (c i) -> p c t i", i=4), func=ACT.Copy,
                 )
         q_codes = [sbt("q_codes%d" % h, [P, PASSES * P], U32) for h in range(QT)]
         q_scales = [sbt("q_scales%d" % h, [P, PASSES * P], U8) for h in range(QT)]
         k_g = [sbt("k_g0", [P, PAGE], U32), placed("k_g1", [P, PAGE], U32, 2)]
-        k_parted = [sbt("k_parted0", [P, PASSES * PAGE * 2], U8), placed("k_parted1", [P, PASSES * PAGE * 2], U8, 6)]
+        k_parted = [sbt("k_parted0", [P, PASSES * PAGE * 2], U8), placed("k_parted1", [P, PASSES * PAGE * 2], U8, 7)]
 
         def gather_keys(g):
             cols = slice(g * PAGE // 16, (g + 1) * PAGE // 16)
@@ -152,7 +147,7 @@ def tile_attend_pkv4_gate_cap_kernel(
         quantize_q(1)
         part_keys(1)
 
-        vsc_g = sbt("vsc_g", [P, PAGES * DV], U8)
+        vsc_g = placed("vsc_g", [P, PAGES * DV], U8, 6)
         nc.vector.tensor_copy(vsc_g[:], vsc_pool[:].indirect(voffs_sb[:]))
         for q in range(QUADS):
             nc.sync.dma_start(

@@ -83,24 +83,23 @@ def tile_attend_pkv4_gate_cap_kernel(
 
         ks_g = sbt("ks_g", [P, N], U8)
         nc.vector.tensor_copy(ks_g[:], ks_pool[:].indirect(offs_sb[:]))
+        vs_g = sbt("vs_g", [P, N], F32)
+        nc.vector.tensor_copy(vs_g[:], vs_pool[:].indirect(offs_sb[:]))
+
+        q_rows = qT[0].rearrange("(o p j) w -> o p j w", o=PASSES, j=PACK)
+        q_raw = [placed("q_raw%d" % o, [P, PACK, NQ], F32, 4 * o) for o in range(PASSES)]
+        for o in range(PASSES):
+            nc.sync.dma_start(q_raw[o][:], q_rows[o])
+        nc.sync.dma_start(voffs_sb[:], voffs)
         for q in range(QUADS):
             nc.sync.dma_start(
                 ks_plane[:].bitcast(I32)[32 * q:32 * q + PACK, :],
                 ks_g[:].bitcast(I32)[96 + 8 * q:96 + 8 * (q + 1), :],
             )
-        vs_g = sbt("vs_g", [P, N], F32)
-        nc.vector.tensor_copy(vs_g[:], vs_pool[:].indirect(offs_sb[:]))
-
-        q_rows = qT[0].rearrange("(o p j) w -> o p j w", o=PASSES, j=PACK)
-        q_raw = [[placed("q_raw%d%d" % (h, o), [P, PACK, P], F32, 4 * h + 2 * o) for o in range(PASSES)] for h in range(QT)]
-        for h in range(QT):
-            for o in range(PASSES):
-                nc.sync.dma_start(q_raw[h][o][:], q_rows[o][:, :, h * P:(h + 1) * P])
         nc.sync.dma_start(
             vsc_pool[:].bitcast(I32)[112:P, :].rearrange("f (u e) -> f u e", u=POOL_PAGES),
             v_scales.rearrange("u f e -> f u e").bitcast(I32),
         )
-        nc.sync.dma_start(voffs_sb[:], voffs)
         vw_pool = sbt("vw_pool", [P, POOL_PAGES * DV], I32)
         nc.sync.dma_start(
             vw_pool[:].rearrange("p (u e) -> p u e", u=POOL_PAGES),
@@ -112,17 +111,17 @@ def tile_attend_pkv4_gate_cap_kernel(
         og_sb = sbt("og_sb", [P, QT, DV], F32)
         nc.sync.dma_start(og_sb[:], og[0].rearrange("(h p) e -> p h e", p=P))
 
-        q_bf = [sbt("q_bf%d" % h, [P, PASSES, P * PACK], BF16) for h in range(QT)]
-        for h in range(QT):
-            for o in range(PASSES):
+        q_bf = [sbt("q_bf%d" % o, [P, QT, P * PACK], BF16) for o in range(PASSES)]
+        for o in range(PASSES):
+            for h in range(QT):
                 nc.scalar.activation(
-                    out=q_bf[h][:, o, :].rearrange("p (c i t) -> p c t i", i=4, t=PACK),
-                    in_=q_raw[h][o][:].rearrange("p t (c i) -> p c t i", i=4), func=ACT.Copy,
+                    out=q_bf[o][:, h, :].rearrange("p (c i t) -> p c t i", i=4, t=PACK),
+                    in_=q_raw[o][:, :, h * P:(h + 1) * P].rearrange("p t (c i) -> p c t i", i=4), func=ACT.Copy,
                 )
-        q_codes = [sbt("q_codes%d" % h, [P, PASSES * P], U32) for h in range(QT)]
-        q_scales = [sbt("q_scales%d" % h, [P, PASSES * P], U8) for h in range(QT)]
-        k_g = [sbt("k_g0", [P, PAGE], U32), placed("k_g1", [P, PAGE], U32, 2)]
-        k_parted = [sbt("k_parted0", [P, PASSES * PAGE * 2], U8), placed("k_parted1", [P, PASSES * PAGE * 2], U8, 7)]
+        q_codes = [sbt("q_codes%d" % o, [P, NQ], U32) for o in range(PASSES)]
+        q_scales = [sbt("q_scales%d" % o, [P, NQ], U8) for o in range(PASSES)]
+        k_g = [sbt("k_g0", [P, PAGE], U32), placed("k_g1", [P, PAGE], U32, 0)]
+        k_parted = [sbt("k_parted0", [P, PASSES * PAGE * 2], U8), placed("k_parted1", [P, PASSES * PAGE * 2], U8, 4)]
 
         def gather_keys(g):
             cols = slice(g * PAGE // 16, (g + 1) * PAGE // 16)
@@ -134,17 +133,18 @@ def tile_attend_pkv4_gate_cap_kernel(
                 k_g[g][:].bitcast(U16).rearrange("p (n o) -> p o n", o=PASSES),
             )
 
-        def quantize_q(h):
+        def quantize_q(o, tiles):
+            cols = slice(tiles.start * P, tiles.stop * P)
             nc.vector.quantize_mx(
-                out=q_codes[h][:].bitcast(FP8X4), scales=q_scales[h][:],
-                in_=q_bf[h][:].rearrange("p o c -> p (o c)"),
+                out=q_codes[o][:, cols].bitcast(FP8X4), scales=q_scales[o][:, cols],
+                in_=q_bf[o][:, tiles, :].rearrange("p h c -> p (h c)"),
             )
 
         gather_keys(0)
         part_keys(0)
-        quantize_q(0)
+        quantize_q(0, slice(0, QT))
         gather_keys(1)
-        quantize_q(1)
+        quantize_q(1, slice(0, QT))
         part_keys(1)
 
         vsc_g = placed("vsc_g", [P, PAGES * DV], U8, 6)
@@ -157,26 +157,33 @@ def tile_attend_pkv4_gate_cap_kernel(
 
         half = [sbt("half%d" % h, [P, N], F32) for h in range(QT)]
         acc = [[bank("score%d%d" % (h, g), "s%d" % (2 * h + g), [P, PAGE]) for g in range(PAGES)] for h in range(QT)]
-        for g in range(PAGES):
-            for h in range(QT):
-                for o in range(PASSES):
-                    nc.tensor.matmul_mx(
-                        out=acc[h][g][:],
-                        lhsT=q_codes[h][:, o * P:(o + 1) * P].bitcast(FP8X4),
-                        lhsT_scale=q_scales[h][:, o * P:(o + 1) * P],
-                        rhs=k_parted[g][:, o * 2 * PAGE:(o + 1) * 2 * PAGE].bitcast(FP4X4),
-                        rhs_scale=ks_plane[:, o * N + g * PAGE:o * N + (g + 1) * PAGE],
-                        start=(o == 0), stop=(o == PASSES - 1),
-                    )
+
+        def score_pass(h, g, o):
+            nc.tensor.matmul_mx(
+                out=acc[h][g][:],
+                lhsT=q_codes[o][:, h * P:(h + 1) * P].bitcast(FP8X4),
+                lhsT_scale=q_scales[o][:, h * P:(h + 1) * P],
+                rhs=k_parted[g][:, o * 2 * PAGE:(o + 1) * 2 * PAGE].bitcast(FP4X4),
+                rhs_scale=ks_plane[:, o * N + g * PAGE:o * N + (g + 1) * PAGE],
+                start=(o == 0), stop=(o == PASSES - 1),
+            )
+            if o == PASSES - 1:
                 nc.scalar.activation(
                     out=half[h][:, g * PAGE:(g + 1) * PAGE].rearrange("p (r s) -> p r s", r=PACK),
                     in_=acc[h][g][:].rearrange("p (s r) -> p r s", r=PACK),
                     func=ACT.Tanh, scale=1.0 / CAP,
                 )
 
+        for o in range(PASSES):
+            for h in range(QT):
+                score_pass(h, 0, o)
+        for h in range(QT):
+            for o in range(PASSES):
+                score_pass(h, 1, o)
+
         neg_c = [[placed("neg_c%d%d" % (h, g), [P, PAGE], F32, 20 + 4 * h + 2 * g) for g in range(PAGES)] for h in range(QT)]
         neg_m = [[sbt("neg_m%d%d" % (h, g), [P, 1], F32) for g in range(PAGES)] for h in range(QT)]
-        prob = [[sbt("prob%d%d" % (h, g), [P, PAGE], F32) for g in range(PAGES)] for h in range(QT)]
+        prob = [[placed("prob%d%d" % (h, g), [P, PAGE], F32, 4 if h + g == 0 else 28 + 4 * h + 2 * g) for g in range(PAGES)] for h in range(QT)]
         part_sum = sbt("part_sum", [P, PAGES, QT], F32)
         row_sum = sbt("row_sum", [P, QT], F32)
         for g in range(PAGES):
@@ -193,6 +200,7 @@ def tile_attend_pkv4_gate_cap_kernel(
                     bias=neg_m[h][PAGES - 1][:], scale=-1.0, accum_out=part_sum[:, g, h:h + 1],
                 )
         nc.gpsimd.tensor_tensor(out=row_sum[:], in0=part_sum[:, 0, :], in1=part_sum[:, 1, :], op=ALU.add)
+
         v_g = placed("v_g", [P, PAGES * DV], U32, 20)
         nc.vector.tensor_copy(v_g[:], vw_pool[:].bitcast(U32).indirect(voffs_sb[:]))
 

@@ -24,7 +24,7 @@ POOL_PAGES = T // PAGE
 PASSES = D // PAGE
 QT = NQ // P
 KIB = 1024
-VS_VECTOR = 1024
+VS_VECTOR = 1280
 FLOPS = 2 * NQ * N * (D + DV)
 BYTES = 4 * D * NQ + 4 * P * T + 2 * 16 * T + 4 * P * DV * POOL_PAGES + 16 * DV * POOL_PAGES + 4 * T + 8 * NQ * DV
 
@@ -56,7 +56,7 @@ def tile_attend_pkv4_gate_cap_kernel(
         offs_sb = lists.tile([P, N // 16], U16, name="offs_sb")
         voffs_sb = lists.tile([P, PAGES * DV // 16], U16, name="voffs_sb")
 
-        ks_pool = sbt("ks_pool", [P, T], U8)
+        ks_pool = placed("ks_pool", [P, T], U8, 12)
         ks_words = ks_pool[:].bitcast(I32)
         vs_pool = sbt("vs_pool", [P, T], F32)
         kw_pool = sbt("kw_pool", [P, T], I32)
@@ -65,21 +65,19 @@ def tile_attend_pkv4_gate_cap_kernel(
         nc.sync.dma_start(vs_pool[P - 1:P, :], vs[0:1, :])
         nc.sync.dma_start(kw_pool[:], k_words[0].rearrange("p t b -> p (t b)").bitcast(I32))
 
-        zero_odd(ks_words[0:96, :])
-        zero_odd(vs_pool[0:P - 1, :VS_VECTOR])
-        nc.gpsimd.memset(vs_pool[0:P - 1, VS_VECTOR:], 0.0)
-        ks_plane = sbt("ks_plane", [P, PASSES * N], U8)
-        nc.gpsimd.memset(ks_plane[:].bitcast(I32), 0)
-        vsc_pool = sbt("vsc_pool", [P, POOL_PAGES * DV], U8)
-        nc.gpsimd.memset(vsc_pool[:].bitcast(I32)[0:112, :], 0)
-        vsc_plane = sbt("vsc_plane", [P, PAGES * DV], U8)
-        nc.gpsimd.memset(vsc_plane[:].bitcast(I32), 0)
         ident = sbt("ident", [P, P], F32)
         nc.gpsimd.memset(ident[:], 0.0)
         nc.gpsimd.affine_select(
             out=ident[:], in_=ident[:], pattern=[[-1, P]], compare_op=ALU.not_equal,
             fill=1.0, base=0, channel_multiplier=1,
         )
+        zero_odd(ks_words[0:96, :])
+        zero_odd(vs_pool[0:P - 1, :VS_VECTOR])
+        nc.gpsimd.memset(vs_pool[0:P - 1, VS_VECTOR:], 0.0)
+        vsc_pool = sbt("vsc_pool", [P, POOL_PAGES * DV], U8)
+        nc.gpsimd.memset(vsc_pool[:].bitcast(I32)[0:112, :], 0)
+        ks_plane = placed("ks_plane", [P, PASSES * N], U8, 12)
+        vsc_plane = placed("vsc_plane", [P, PAGES * DV], U8, 14)
 
         ks_g = sbt("ks_g", [P, N], U8)
         nc.vector.tensor_copy(ks_g[:], ks_pool[:].indirect(offs_sb[:]))

@@ -109,16 +109,16 @@ def tile_attend_pkv4_gate_cap_kernel(
         og_sb = sbt("og_sb", [P, QT, DV], F32)
         nc.sync.dma_start(og_sb[:], og[0].rearrange("(h p) e -> p h e", p=P))
 
-        q_bf = [sbt("q_bf%d" % o, [P, QT, P * PACK], BF16) for o in range(PASSES)]
+        q_bf = [sbt("q_bf%d" % h, [P, PASSES, P * PACK], BF16) for h in range(QT)]
         for o in range(PASSES):
             for h in range(QT):
                 nc.scalar.activation(
-                    out=q_bf[o][:, h, :].rearrange("p (c i t) -> p c t i", i=4, t=PACK),
+                    out=q_bf[h][:, o, :].rearrange("p (c i t) -> p c t i", i=4, t=PACK),
                     in_=q_raw[o][:, :, h * P:(h + 1) * P].rearrange("p t (c i) -> p c t i", i=4), func=ACT.Copy,
                 )
-        q_codes = [sbt("q_codes%d" % o, [P, NQ], U32) for o in range(PASSES)]
-        q_scales = [sbt("q_scales%d" % o, [P, NQ], U8) for o in range(PASSES)]
-        k_g = [sbt("k_g0", [P, PAGE], U32), placed("k_g1", [P, PAGE], U32, 0)]
+        q_codes = [sbt("q_codes%d" % h, [P, PASSES * P], U32) for h in range(QT)]
+        q_scales = [sbt("q_scales%d" % h, [P, PASSES * P], U8) for h in range(QT)]
+        k_g = [sbt("k_g%d" % g, [P, PAGE], U32) for g in range(PAGES)]
         k_parted = [sbt("k_parted0", [P, PASSES * PAGE * 2], U8), placed("k_parted1", [P, PASSES * PAGE * 2], U8, 4)]
 
         def gather_keys(g):
@@ -131,18 +131,19 @@ def tile_attend_pkv4_gate_cap_kernel(
                 k_g[g][:].bitcast(U16).rearrange("p (n o) -> p o n", o=PASSES),
             )
 
-        def quantize_q(o, tiles):
-            cols = slice(tiles.start * P, tiles.stop * P)
+        def quantize_q(h, passes):
+            cols = slice(passes.start * P, passes.stop * P)
             nc.vector.quantize_mx(
-                out=q_codes[o][:, cols].bitcast(FP8X4), scales=q_scales[o][:, cols],
-                in_=q_bf[o][:, tiles, :].rearrange("p h c -> p (h c)"),
+                out=q_codes[h][:, cols].bitcast(FP8X4), scales=q_scales[h][:, cols],
+                in_=q_bf[h][:, passes, :].rearrange("p o c -> p (o c)"),
             )
 
         gather_keys(0)
         part_keys(0)
-        quantize_q(0, slice(0, QT))
         gather_keys(1)
-        quantize_q(1, slice(0, QT))
+        for o in range(PASSES):
+            quantize_q(0, slice(o, o + 1))
+        quantize_q(1, slice(0, PASSES))
         part_keys(1)
 
         vsc_g = placed("vsc_g", [P, PAGES * DV], U8, 6)
@@ -159,8 +160,8 @@ def tile_attend_pkv4_gate_cap_kernel(
         def score_pass(h, g, o):
             nc.tensor.matmul_mx(
                 out=acc[h][g][:],
-                lhsT=q_codes[o][:, h * P:(h + 1) * P].bitcast(FP8X4),
-                lhsT_scale=q_scales[o][:, h * P:(h + 1) * P],
+                lhsT=q_codes[h][:, o * P:(o + 1) * P].bitcast(FP8X4),
+                lhsT_scale=q_scales[h][:, o * P:(o + 1) * P],
                 rhs=k_parted[g][:, o * 2 * PAGE:(o + 1) * 2 * PAGE].bitcast(FP4X4),
                 rhs_scale=ks_plane[:, o * N + g * PAGE:o * N + (g + 1) * PAGE],
                 start=(o == 0), stop=(o == PASSES - 1),
@@ -172,12 +173,10 @@ def tile_attend_pkv4_gate_cap_kernel(
                     func=ACT.Tanh, scale=1.0 / CAP,
                 )
 
-        for o in range(PASSES):
+        for g in range(PAGES):
             for h in range(QT):
-                score_pass(h, 0, o)
-        for h in range(QT):
-            for o in range(PASSES):
-                score_pass(h, 1, o)
+                for o in range(PASSES):
+                    score_pass(h, g, o)
 
         neg_c = [[placed("neg_c%d%d" % (h, g), [P, PAGE], F32, 20 + 4 * h + 2 * g) for g in range(PAGES)] for h in range(QT)]
         neg_m = [[sbt("neg_m%d%d" % (h, g), [P, 1], F32) for g in range(PAGES)] for h in range(QT)]

@@ -60,8 +60,8 @@ def tile_attend_pkv4_gate_cap_kernel(
         ks_words = ks_pool[:].bitcast(I32)
         vs_pool = sbt("vs_pool", [P, T], F32)
         kw_pool = sbt("kw_pool", [P, T], I32)
-        nc.sync.dma_start(offs_sb[:], offs)
         nc.sync.dma_start(ks_words[96:P, :], k_scales.rearrange("o r t -> r o t").bitcast(I32))
+        nc.sync.dma_start(offs_sb[:], offs)
         nc.sync.dma_start(vs_pool[P - 1:P, :], vs[0:1, :])
         nc.sync.dma_start(kw_pool[:], k_words[0].rearrange("p t b -> p (t b)").bitcast(I32))
 
@@ -89,7 +89,7 @@ def tile_attend_pkv4_gate_cap_kernel(
         for o in range(PASSES):
             nc.sync.dma_start(q_raw[o][:], q_rows[o])
         nc.sync.dma_start(voffs_sb[:], voffs)
-        for q in range(QUADS):
+        for q in (0, 2, 1, 3):
             nc.sync.dma_start(
                 ks_plane[:].bitcast(I32)[32 * q:32 * q + PACK, :],
                 ks_g[:].bitcast(I32)[96 + 8 * q:96 + 8 * (q + 1), :],

@@ -76,7 +76,7 @@ def tile_attend_pkv4_gate_cap_kernel(
         nc.gpsimd.memset(vs_pool[0:P - 1, VS_VECTOR:], 0.0)
         vsc_pool = sbt("vsc_pool", [P, POOL_PAGES * DV], U8)
         nc.gpsimd.memset(vsc_pool[:].bitcast(I32)[0:112, :], 0)
-        ks_plane = placed("ks_plane", [P, PASSES * N], U8, 12)
+        ks_plane = [placed("ks_plane%d" % g, [P, PASSES * PAGE], U8, 12 + g) for g in range(PAGES)]
         vsc_plane = placed("vsc_plane", [P, PAGES * DV], U8, 14)
 
         ks_g = sbt("ks_g", [P, N], U8)
@@ -86,18 +86,23 @@ def tile_attend_pkv4_gate_cap_kernel(
 
         q_rows = qT[0].rearrange("(o p j) w -> o p j w", o=PASSES, j=PACK)
         q_raw = [placed("q_raw%d" % o, [P, PACK, NQ], F32, 4 * o) for o in range(PASSES)]
-        for o in range(PASSES):
-            nc.sync.dma_start(q_raw[o][:], q_rows[o])
+
+        def move_key_planes(g):
+            for q in (0, 2, 1, 3):
+                nc.sync.dma_start(
+                    ks_plane[g][:].bitcast(I32)[32 * q:32 * q + PACK, :],
+                    ks_g[:, g * PAGE:(g + 1) * PAGE].bitcast(I32)[96 + 8 * q:96 + 8 * (q + 1), :],
+                )
+
+        nc.sync.dma_start(q_raw[0][:], q_rows[0])
+        move_key_planes(0)
+        nc.sync.dma_start(q_raw[1][:], q_rows[1])
         nc.sync.dma_start(voffs_sb[:], voffs)
-        for q in (0, 2, 1, 3):
-            nc.sync.dma_start(
-                ks_plane[:].bitcast(I32)[32 * q:32 * q + PACK, :],
-                ks_g[:].bitcast(I32)[96 + 8 * q:96 + 8 * (q + 1), :],
-            )
         nc.sync.dma_start(
             vsc_pool[:].bitcast(I32)[112:P, :].rearrange("f (u e) -> f u e", u=POOL_PAGES),
             v_scales.rearrange("u f e -> f u e").bitcast(I32),
         )
+        move_key_planes(1)
         vw_pool = sbt("vw_pool", [P, POOL_PAGES * DV], I32)
         nc.sync.dma_start(
             vw_pool[:].rearrange("p (u e) -> p u e", u=POOL_PAGES),
@@ -119,7 +124,7 @@ def tile_attend_pkv4_gate_cap_kernel(
         q_codes = [sbt("q_codes%d" % h, [P, PASSES * P], U32) for h in range(QT)]
         q_scales = [sbt("q_scales%d" % h, [P, PASSES * P], U8) for h in range(QT)]
         k_g = [sbt("k_g%d" % g, [P, PAGE], U32) for g in range(PAGES)]
-        k_parted = [sbt("k_parted0", [P, PASSES * PAGE * 2], U8), placed("k_parted1", [P, PASSES * PAGE * 2], U8, 4)]
+        k_parted = [sbt("k_parted0", [P, PASSES * PAGE * 2], U8), placed("k_parted1", [P, PASSES * PAGE * 2], U8, 0)]
 
         def gather_keys(g):
             cols = slice(g * PAGE // 16, (g + 1) * PAGE // 16)
@@ -139,12 +144,13 @@ def tile_attend_pkv4_gate_cap_kernel(
             )
 
         gather_keys(0)
-        part_keys(0)
         gather_keys(1)
-        for o in range(PASSES):
-            quantize_q(0, slice(o, o + 1))
-        quantize_q(1, slice(0, PASSES))
+        part_keys(0)
+        for h in range(QT):
+            quantize_q(h, slice(0, 1))
         part_keys(1)
+        for h in range(QT):
+            quantize_q(h, slice(1, PASSES))
 
         vsc_g = placed("vsc_g", [P, PAGES * DV], U8, 6)
         nc.vector.tensor_copy(vsc_g[:], vsc_pool[:].indirect(voffs_sb[:]))
@@ -163,7 +169,7 @@ def tile_attend_pkv4_gate_cap_kernel(
                 lhsT=q_codes[h][:, o * P:(o + 1) * P].bitcast(FP8X4),
                 lhsT_scale=q_scales[h][:, o * P:(o + 1) * P],
                 rhs=k_parted[g][:, o * 2 * PAGE:(o + 1) * 2 * PAGE].bitcast(FP4X4),
-                rhs_scale=ks_plane[:, o * N + g * PAGE:o * N + (g + 1) * PAGE],
+                rhs_scale=ks_plane[g][:, o * PAGE:(o + 1) * PAGE],
                 start=(o == 0), stop=(o == PASSES - 1),
             )
             if o == PASSES - 1:
@@ -173,14 +179,16 @@ def tile_attend_pkv4_gate_cap_kernel(
                     func=ACT.Tanh, scale=1.0 / CAP,
                 )
 
-        for g in range(PAGES):
+        for o in range(PASSES):
             for h in range(QT):
-                for o in range(PASSES):
-                    score_pass(h, g, o)
+                score_pass(h, 0, o)
+        for h in range(QT):
+            for o in range(PASSES):
+                score_pass(h, 1, o)
 
         neg_c = [[placed("neg_c%d%d" % (h, g), [P, PAGE], F32, 20 + 4 * h + 2 * g) for g in range(PAGES)] for h in range(QT)]
         neg_m = [[sbt("neg_m%d%d" % (h, g), [P, 1], F32) for g in range(PAGES)] for h in range(QT)]
-        prob = [[placed("prob%d%d" % (h, g), [P, PAGE], F32, 4 if h + g == 0 else 28 + 4 * h + 2 * g) for g in range(PAGES)] for h in range(QT)]
+        prob = [[placed("prob%d%d" % (h, g), [P, PAGE], F32, 0 if h + g == 0 else 28 + 4 * h + 2 * g) for g in range(PAGES)] for h in range(QT)]
         part_sum = sbt("part_sum", [P, PAGES, QT], F32)
         row_sum = sbt("row_sum", [P, QT], F32)
         for g in range(PAGES):

@@ -24,7 +24,8 @@ POOL_PAGES = T // PAGE
 PASSES = D // PAGE
 QT = NQ // P
 KIB = 1024
-VS_VECTOR = 1280
+HALF = T // 2
+VS_VECTOR = 1792
 FLOPS = 2 * NQ * N * (D + DV)
 BYTES = 4 * D * NQ + 4 * P * T + 2 * 16 * T + 4 * P * DV * POOL_PAGES + 16 * DV * POOL_PAGES + 4 * T + 8 * NQ * DV
 
@@ -62,20 +63,23 @@ def tile_attend_pkv4_gate_cap_kernel(
         kw_pool = sbt("kw_pool", [P, T], I32)
         nc.sync.dma_start(ks_words[96:P, :], k_scales.rearrange("o r t -> r o t").bitcast(I32))
         nc.sync.dma_start(offs_sb[:], offs)
-        nc.sync.dma_start(vs_pool[P - 1:P, :], vs[0:1, :])
+        nc.sync.dma_start(vs_pool[P // 2 - 1:P // 2, :HALF], vs[0:1, :HALF])
+        nc.sync.dma_start(vs_pool[P - 1:P, HALF:], vs[0:1, HALF:])
         nc.sync.dma_start(kw_pool[:], k_words[0].rearrange("p t b -> p (t b)").bitcast(I32))
 
+        zero_odd(ks_words[0:96, :])
+        zero_odd(vs_pool[0:P // 2 - 1, :VS_VECTOR])
+        nc.gpsimd.memset(vs_pool[0:P // 2 - 1, VS_VECTOR:HALF], 0.0)
+        nc.gpsimd.memset(vs_pool[P // 2:P, :HALF], 0.0)
+        nc.gpsimd.memset(vs_pool[0:P - 1, HALF:], 0.0)
+        vsc_pool = sbt("vsc_pool", [P, POOL_PAGES * DV], U8)
+        nc.gpsimd.memset(vsc_pool[:].bitcast(I32)[0:112, :], 0)
         ident = sbt("ident", [P, P], F32)
         nc.gpsimd.memset(ident[:], 0.0)
         nc.gpsimd.affine_select(
             out=ident[:], in_=ident[:], pattern=[[-1, P]], compare_op=ALU.not_equal,
             fill=1.0, base=0, channel_multiplier=1,
         )
-        zero_odd(ks_words[0:96, :])
-        zero_odd(vs_pool[0:P - 1, :VS_VECTOR])
-        nc.gpsimd.memset(vs_pool[0:P - 1, VS_VECTOR:], 0.0)
-        vsc_pool = sbt("vsc_pool", [P, POOL_PAGES * DV], U8)
-        nc.gpsimd.memset(vsc_pool[:].bitcast(I32)[0:112, :], 0)
         ks_plane = [placed("ks_plane%d" % g, [P, PASSES * PAGE], U8, 12 + g) for g in range(PAGES)]
         vsc_plane = placed("vsc_plane", [P, PAGES * DV], U8, 14)
 
@@ -108,9 +112,13 @@ def tile_attend_pkv4_gate_cap_kernel(
             vw_pool[:].rearrange("p (u e) -> p u e", u=POOL_PAGES),
             v_words.rearrange("u p e b -> p u (e b)").bitcast(I32),
         )
-        vs_col = [sbt("vs_col%d" % g, [P, PACK], F32) for g in range(PAGES)]
-        for g in range(PAGES):
-            nc.sync.dma_start(vs_col[g][:], vs_g[P - 1:P, g * PAGE:(g + 1) * PAGE])
+        parts = [placed("vs_part%d" % a, [P, PAGES, 2 * PACK], F32, 16 + a) for a in range(2)]
+        for a in range(2):
+            row = (a + 1) * P // 2 - 1
+            for g in range(PAGES):
+                nc.sync.dma_start(parts[a][:, g, :PACK], vs_g[row:row + 1, g * PAGE:(g + 1) * PAGE])
+        vs_col = sbt("vs_col", [P, PAGES, PACK], F32)
+        nc.gpsimd.tensor_tensor(out=vs_col[:], in0=parts[0][:, :, :PACK], in1=parts[1][:, :, :PACK], op=ALU.add)
         og_sb = sbt("og_sb", [P, QT, DV], F32)
         nc.sync.dma_start(og_sb[:], og[0].rearrange("(h p) e -> p h e", p=P))
 
@@ -190,7 +198,7 @@ def tile_attend_pkv4_gate_cap_kernel(
         neg_m = [[sbt("neg_m%d%d" % (h, g), [P, 1], F32) for g in range(PAGES)] for h in range(QT)]
         prob = [[placed("prob%d%d" % (h, g), [P, PAGE], F32, 0 if h + g == 0 else 28 + 4 * h + 2 * g) for g in range(PAGES)] for h in range(QT)]
         part_sum = sbt("part_sum", [P, PAGES, QT], F32)
-        row_sum = sbt("row_sum", [P, QT], F32)
+        row_sum = placed("row_sum", [P, QT], F32, 16)
         for g in range(PAGES):
             for h in range(QT):
                 nc.vector.tensor_scalar(
@@ -224,7 +232,7 @@ def tile_attend_pkv4_gate_cap_kernel(
                 nc.tensor.transpose(p_t[:, r, :], prob[h][g][:, r * P:(r + 1) * P], ident[:])
             nc.vector.tensor_tensor(
                 out=w_bf[h][:, g], in0=p_t[:].rearrange("p r q -> p q r"),
-                in1=vs_col[g][:].unsqueeze(1).to_broadcast([P, P, PACK]), op=ALU.mult,
+                in1=vs_col[:, g, :].unsqueeze(1).to_broadcast([P, P, PACK]), op=ALU.mult,
             )
 
         def quantize_w(h, pages):

@@ -198,6 +198,7 @@ def tile_attend_pkv4_gate_cap_kernel(
         neg_m = [[sbt("neg_m%d%d" % (h, g), [P, 1], F32) for g in range(PAGES)] for h in range(QT)]
         prob = [[placed("prob%d%d" % (h, g), [P, PAGE], F32, 0 if h + g == 0 else 28 + 4 * h + 2 * g) for g in range(PAGES)] for h in range(QT)]
         part_sum = sbt("part_sum", [P, PAGES, QT], F32)
+        first_sum = sbt("first_sum", [P, 2], F32)
         row_sum = placed("row_sum", [P, QT], F32, 16)
         for g in range(PAGES):
             for h in range(QT):
@@ -206,15 +207,23 @@ def tile_attend_pkv4_gate_cap_kernel(
                     scalar2=neg_m[h][0][:] if g else None,
                     op0=ALU.mult, op1=ALU.min, accum_out=neg_m[h][g][:],
                 )
-        for h in range(QT):
-            for g in range(PAGES):
-                nc.scalar.activation(
-                    out=prob[h][g][:], in_=neg_c[h][g][:], func=ACT.Exp,
-                    bias=neg_m[h][PAGES - 1][:], scale=-1.0, accum_out=part_sum[:, g, h:h + 1],
-                )
-        nc.gpsimd.tensor_tensor(out=row_sum[:], in0=part_sum[:, 0, :], in1=part_sum[:, 1, :], op=ALU.add)
 
-        v_g = placed("v_g", [P, PAGES * DV], U32, 20)
+        def weights(h, g, cols, total):
+            nc.scalar.activation(
+                out=prob[h][g][:, cols], in_=neg_c[h][g][:, cols], func=ACT.Exp,
+                bias=neg_m[h][PAGES - 1][:], scale=-1.0, accum_out=total,
+            )
+
+        for a in range(2):
+            weights(0, 0, slice(a * PAGE // 2, (a + 1) * PAGE // 2), first_sum[:, a:a + 1])
+        joined = placed("joined", [P, 1], F32, 17)
+        nc.gpsimd.tensor_tensor(out=joined[:], in0=first_sum[:, 0:1], in1=first_sum[:, 1:2], op=ALU.add)
+        for h, g in ((0, 1), (1, 0), (1, 1)):
+            weights(h, g, slice(0, PAGE), part_sum[:, g, h:h + 1])
+        for h, page0 in enumerate((joined[:], part_sum[:, 0, 1:2])):
+            nc.gpsimd.tensor_tensor(out=row_sum[:, h:h + 1], in0=page0, in1=part_sum[:, 1, h:h + 1], op=ALU.add)
+
+        v_g = sbt("v_g", [P, PAGES * DV], U32)
         nc.vector.tensor_copy(v_g[:], vw_pool[:].bitcast(U32).indirect(voffs_sb[:]))
 
         gate_t = placed("gate_t", [P, QT, DV], F32, 26)
@@ -242,25 +251,29 @@ def tile_attend_pkv4_gate_cap_kernel(
                 in_=w_bf[h][:, pages].rearrange("p g q r -> p (g q r)"),
             )
 
-        y = [bank("y%d" % h, "s%d" % h, [P, DV]) for h in range(QT)]
+        pieces = [(0, 0, DV), (1, 0, DV // 2), (1, DV // 2, DV)]
+        y = [bank("y%d" % i, "s%d" % i, [P, hi - lo]) for i, (h, lo, hi) in enumerate(pieces)]
 
-        def value_pass(h, g):
+        def value_pass(i, g):
+            h, lo, hi = pieces[i]
+            cols = slice(g * DV + lo, g * DV + hi)
             nc.tensor.matmul_mx(
-                out=y[h][:],
+                out=y[i][:],
                 lhsT=w_codes[h][:, g * P:(g + 1) * P].bitcast(FP8X4), lhsT_scale=w_scales[h][:, g * P:(g + 1) * P],
-                rhs=v_g[:, g * DV:(g + 1) * DV].bitcast(FP8X4), rhs_scale=vsc_plane[:, g * DV:(g + 1) * DV],
+                rhs=v_g[:, cols].bitcast(FP8X4), rhs_scale=vsc_plane[:, cols],
                 start=(g == 0), stop=(g == PAGES - 1),
             )
 
         inv_sum = sbt("inv_sum", [P, QT], F32)
 
-        def finish(h):
-            res = sbt("res%d" % h, [P, DV], F32)
+        def finish(i):
+            h, lo, hi = pieces[i]
+            res = sbt("res%d" % i, [P, hi - lo], F32)
             nc.vector.scalar_tensor_tensor(
-                out=res[:], in0=y[h][:], scalar=inv_sum[:, h:h + 1], in1=gate[:, h, :],
+                out=res[:], in0=y[i][:], scalar=inv_sum[:, h:h + 1], in1=gate[:, h, lo:hi],
                 op0=ALU.mult, op1=ALU.mult,
             )
-            nc.sync.dma_start(out[0, h * P:(h + 1) * P, :], res[:])
+            nc.sync.dma_start(out[0, h * P:(h + 1) * P, lo:hi], res[:])
 
         weigh(0, 0)
         weigh(0, 1)
@@ -272,7 +285,8 @@ def tile_attend_pkv4_gate_cap_kernel(
         quantize_w(1, slice(0, 1))
         nc.vector.reciprocal(inv_sum[:], row_sum[:])
         quantize_w(1, slice(1, PAGES))
-        value_pass(1, 0)
-        value_pass(1, 1)
-        finish(0)
-        finish(1)
+        for g in range(PAGES):
+            value_pass(1, g)
+            value_pass(2, g)
+        for i in range(len(pieces)):
+            finish(i)

@@ -24,8 +24,7 @@ POOL_PAGES = T // PAGE
 PASSES = D // PAGE
 QT = NQ // P
 KIB = 1024
-HALF = T // 2
-VS_VECTOR = 1792
+VS_CUT = 1792
 FLOPS = 2 * NQ * N * (D + DV)
 BYTES = 4 * D * NQ + 4 * P * T + 2 * 16 * T + 4 * P * DV * POOL_PAGES + 16 * DV * POOL_PAGES + 4 * T + 8 * NQ * DV
 
@@ -63,15 +62,14 @@ def tile_attend_pkv4_gate_cap_kernel(
         kw_pool = sbt("kw_pool", [P, T], I32)
         nc.sync.dma_start(ks_words[96:P, :], k_scales.rearrange("o r t -> r o t").bitcast(I32))
         nc.sync.dma_start(offs_sb[:], offs)
-        nc.sync.dma_start(vs_pool[P // 2 - 1:P // 2, :HALF], vs[0:1, :HALF])
-        nc.sync.dma_start(vs_pool[P - 1:P, HALF:], vs[0:1, HALF:])
+        nc.sync.dma_start(vs_pool[P // 2 - 1:P // 2, :VS_CUT], vs[0:1, :VS_CUT])
+        nc.sync.dma_start(vs_pool[P - 1:P, VS_CUT:], vs[0:1, VS_CUT:])
         nc.sync.dma_start(kw_pool[:], k_words[0].rearrange("p t b -> p (t b)").bitcast(I32))
 
         zero_odd(ks_words[0:96, :])
-        zero_odd(vs_pool[0:P // 2 - 1, :VS_VECTOR])
-        nc.gpsimd.memset(vs_pool[0:P // 2 - 1, VS_VECTOR:HALF], 0.0)
-        nc.gpsimd.memset(vs_pool[P // 2:P, :HALF], 0.0)
-        nc.gpsimd.memset(vs_pool[0:P - 1, HALF:], 0.0)
+        zero_odd(vs_pool[0:P // 2 - 1, :VS_CUT])
+        nc.gpsimd.memset(vs_pool[P // 2:P, :VS_CUT], 0.0)
+        nc.gpsimd.memset(vs_pool[0:P - 1, VS_CUT:], 0.0)
         vsc_pool = sbt("vsc_pool", [P, POOL_PAGES * DV], U8)
         nc.gpsimd.memset(vsc_pool[:].bitcast(I32)[0:112, :], 0)
         ident = sbt("ident", [P, P], F32)
@@ -140,8 +138,8 @@ def tile_attend_pkv4_gate_cap_kernel(
 
         def part_keys(g):
             nc.vector.tensor_copy(
-                k_parted[g][:].bitcast(U16).rearrange("p (o n) -> p o n", o=PASSES),
-                k_g[g][:].bitcast(U16).rearrange("p (n o) -> p o n", o=PASSES),
+                k_parted[g][:].bitcast(U16).rearrange("p (o a n) -> p a o n", o=PASSES, a=2),
+                k_g[g][:].bitcast(U16).rearrange("p (a n o) -> p a o n", o=PASSES, a=2),
             )
 
         def quantize_q(h, passes):
@@ -240,8 +238,9 @@ def tile_attend_pkv4_gate_cap_kernel(
             for r in range(PACK):
                 nc.tensor.transpose(p_t[:, r, :], prob[h][g][:, r * P:(r + 1) * P], ident[:])
             nc.vector.tensor_tensor(
-                out=w_bf[h][:, g], in0=p_t[:].rearrange("p r q -> p q r"),
-                in1=vs_col[:, g, :].unsqueeze(1).to_broadcast([P, P, PACK]), op=ALU.mult,
+                out=w_bf[h][:, g].rearrange("p (c e) r -> p c r e", e=2),
+                in0=p_t[:].rearrange("p r (c e) -> p c r e", e=2),
+                in1=vs_col[:, g, :].unsqueeze(1).unsqueeze(3).to_broadcast([P, P // 2, PACK, 2]), op=ALU.mult,
             )
 
         def quantize_w(h, pages):

@@ -197,7 +197,7 @@ def tile_attend_pkv4_gate_cap_kernel(
         prob = [[placed("prob%d%d" % (h, g), [P, PAGE], F32, 0 if h + g == 0 else 28 + 4 * h + 2 * g) for g in range(PAGES)] for h in range(QT)]
         part_sum = sbt("part_sum", [P, PAGES, QT], F32)
         first_sum = sbt("first_sum", [P, 2], F32)
-        row_sum = placed("row_sum", [P, QT], F32, 16)
+        row_sum = sbt("row_sum", [P, QT], F32)
         for g in range(PAGES):
             for h in range(QT):
                 nc.vector.tensor_scalar(
@@ -214,12 +214,12 @@ def tile_attend_pkv4_gate_cap_kernel(
 
         for a in range(2):
             weights(0, 0, slice(a * PAGE // 2, (a + 1) * PAGE // 2), first_sum[:, a:a + 1])
-        joined = placed("joined", [P, 1], F32, 17)
-        nc.gpsimd.tensor_tensor(out=joined[:], in0=first_sum[:, 0:1], in1=first_sum[:, 1:2], op=ALU.add)
         for h, g in ((0, 1), (1, 0), (1, 1)):
             weights(h, g, slice(0, PAGE), part_sum[:, g, h:h + 1])
-        for h, page0 in enumerate((joined[:], part_sum[:, 0, 1:2])):
-            nc.gpsimd.tensor_tensor(out=row_sum[:, h:h + 1], in0=page0, in1=part_sum[:, 1, h:h + 1], op=ALU.add)
+        joined = sbt("joined", [P, 1], F32)
+        nc.scalar.activation(out=joined[:], in_=first_sum[:, 0:1], func=ACT.Identity, bias=first_sum[:, 1:2])
+        for h, page0 in ((1, part_sum[:, 0, 1:2]), (0, joined[:])):
+            nc.scalar.activation(out=row_sum[:, h:h + 1], in_=page0, func=ACT.Identity, bias=part_sum[:, 1, h:h + 1])
 
         v_g = sbt("v_g", [P, PAGES * DV], U32)
         nc.vector.tensor_copy(v_g[:], vw_pool[:].bitcast(U32).indirect(voffs_sb[:]))

@@ -24,7 +24,6 @@ POOL_PAGES = T // PAGE
 PASSES = D // PAGE
 QT = NQ // P
 KIB = 1024
-VS_CUT = 1792
 FLOPS = 2 * NQ * N * (D + DV)
 BYTES = 4 * D * NQ + 4 * P * T + 2 * 16 * T + 4 * P * DV * POOL_PAGES + 16 * DV * POOL_PAGES + 4 * T + 8 * NQ * DV
 
@@ -60,16 +59,14 @@ def tile_attend_pkv4_gate_cap_kernel(
         ks_words = ks_pool[:].bitcast(I32)
         vs_pool = sbt("vs_pool", [P, T], F32)
         kw_pool = sbt("kw_pool", [P, T], I32)
-        nc.sync.dma_start(ks_words[96:P, :], k_scales.rearrange("o r t -> r o t").bitcast(I32))
+        nc.sync.dma_start(ks_words[32:64, :], k_scales.rearrange("o r t -> r o t").bitcast(I32))
         nc.sync.dma_start(offs_sb[:], offs)
-        nc.sync.dma_start(vs_pool[P // 2 - 1:P // 2, :VS_CUT], vs[0:1, :VS_CUT])
-        nc.sync.dma_start(vs_pool[P - 1:P, VS_CUT:], vs[0:1, VS_CUT:])
+        nc.sync.dma_start(vs_pool[P - 1:P, :], vs[0:1, :])
         nc.sync.dma_start(kw_pool[:], k_words[0].rearrange("p t b -> p (t b)").bitcast(I32))
 
-        zero_odd(ks_words[0:96, :])
-        zero_odd(vs_pool[0:P // 2 - 1, :VS_CUT])
-        nc.gpsimd.memset(vs_pool[P // 2:P, :VS_CUT], 0.0)
-        nc.gpsimd.memset(vs_pool[0:P - 1, VS_CUT:], 0.0)
+        zero_odd(ks_words[0:32, :])
+        zero_odd(ks_words[64:P, :])
+        nc.gpsimd.memset(vs_pool[0:P - 1, :], 0.0)
         vsc_pool = sbt("vsc_pool", [P, POOL_PAGES * DV], U8)
         nc.gpsimd.memset(vsc_pool[:].bitcast(I32)[0:112, :], 0)
         ident = sbt("ident", [P, P], F32)
@@ -93,7 +90,7 @@ def tile_attend_pkv4_gate_cap_kernel(
             for q in (0, 2, 1, 3):
                 nc.sync.dma_start(
                     ks_plane[g][:].bitcast(I32)[32 * q:32 * q + PACK, :],
-                    ks_g[:, g * PAGE:(g + 1) * PAGE].bitcast(I32)[96 + 8 * q:96 + 8 * (q + 1), :],
+                    ks_g[:, g * PAGE:(g + 1) * PAGE].bitcast(I32)[32 + 8 * q:32 + 8 * (q + 1), :],
                 )
 
         nc.sync.dma_start(q_raw[0][:], q_rows[0])
@@ -110,13 +107,9 @@ def tile_attend_pkv4_gate_cap_kernel(
             vw_pool[:].rearrange("p (u e) -> p u e", u=POOL_PAGES),
             v_words.rearrange("u p e b -> p u (e b)").bitcast(I32),
         )
-        parts = [placed("vs_part%d" % a, [P, PAGES, 2 * PACK], F32, 16 + a) for a in range(2)]
-        for a in range(2):
-            row = (a + 1) * P // 2 - 1
-            for g in range(PAGES):
-                nc.sync.dma_start(parts[a][:, g, :PACK], vs_g[row:row + 1, g * PAGE:(g + 1) * PAGE])
-        vs_col = sbt("vs_col", [P, PAGES, PACK], F32)
-        nc.gpsimd.tensor_tensor(out=vs_col[:], in0=parts[0][:, :, :PACK], in1=parts[1][:, :, :PACK], op=ALU.add)
+        vs_col = [sbt("vs_col%d" % g, [P, PACK], F32) for g in range(PAGES)]
+        for g in (1, 0):
+            nc.sync.dma_start(vs_col[g][:], vs_g[P - 1:P, g * PAGE:(g + 1) * PAGE])
         og_sb = sbt("og_sb", [P, QT, DV], F32)
         nc.sync.dma_start(og_sb[:], og[0].rearrange("(h p) e -> p h e", p=P))
 
@@ -230,7 +223,7 @@ def tile_attend_pkv4_gate_cap_kernel(
         nc.scalar.activation(out=gate[:], in_=gate_t[:], func=ACT.Copy, scale=0.5, bias=0.5)
 
         w_bf = [sbt("w_bf%d" % h, [P, PAGES, P, PACK], BF16) for h in range(QT)]
-        w_codes = [sbt("w_codes%d" % h, [P, PAGES * P], U32) for h in range(QT)]
+        w_codes = [placed("w_codes%d" % h, [P, PAGES * P], U32, 32 + 2 * h) for h in range(QT)]
         w_scales = [sbt("w_scales%d" % h, [P, PAGES * P], U8) for h in range(QT)]
 
         def weigh(h, g):
@@ -240,7 +233,7 @@ def tile_attend_pkv4_gate_cap_kernel(
             nc.vector.tensor_tensor(
                 out=w_bf[h][:, g].rearrange("p (c e) r -> p c r e", e=2),
                 in0=p_t[:].rearrange("p r (c e) -> p c r e", e=2),
-                in1=vs_col[:, g, :].unsqueeze(1).unsqueeze(3).to_broadcast([P, P // 2, PACK, 2]), op=ALU.mult,
+                in1=vs_col[g][:].unsqueeze(1).unsqueeze(3).to_broadcast([P, P // 2, PACK, 2]), op=ALU.mult,
             )
 
         def quantize_w(h, pages):

@@ -86,22 +86,22 @@ def tile_attend_pkv4_gate_cap_kernel(
         q_rows = qT[0].rearrange("(o p j) w -> o p j w", o=PASSES, j=PACK)
         q_raw = [placed("q_raw%d" % o, [P, PACK, NQ], F32, 4 * o) for o in range(PASSES)]
 
-        def move_key_planes(g):
+        def move_key_planes(g, queue):
             for q in (0, 2, 1, 3):
-                nc.sync.dma_start(
+                queue.dma_start(
                     ks_plane[g][:].bitcast(I32)[32 * q:32 * q + PACK, :],
                     ks_g[:, g * PAGE:(g + 1) * PAGE].bitcast(I32)[32 + 8 * q:32 + 8 * (q + 1), :],
                 )
 
         nc.sync.dma_start(q_raw[0][:], q_rows[0])
-        move_key_planes(0)
+        move_key_planes(0, nc.scalar)
         nc.sync.dma_start(q_raw[1][:], q_rows[1])
         nc.sync.dma_start(voffs_sb[:], voffs)
         nc.sync.dma_start(
             vsc_pool[:].bitcast(I32)[112:P, :].rearrange("f (u e) -> f u e", u=POOL_PAGES),
             v_scales.rearrange("u f e -> f u e").bitcast(I32),
         )
-        move_key_planes(1)
+        move_key_planes(1, nc.sync)
         vw_pool = sbt("vw_pool", [P, POOL_PAGES * DV], I32)
         nc.sync.dma_start(
             vw_pool[:].rearrange("p (u e) -> p u e", u=POOL_PAGES),

from contextlib import ExitStack

import concourse.mybir as mybir

F32 = mybir.dt.float32
BF16 = mybir.dt.bfloat16
I32 = mybir.dt.int32
U32 = mybir.dt.uint32
U16 = mybir.dt.uint16
U8 = mybir.dt.uint8
FP8X4 = mybir.dt.float8_e4m3fn_x4
FP4X4 = mybir.dt.float4_e2m1fn_x4
ACT = mybir.ActivationFunctionType
ALU = mybir.AluOpType

P = 128
PACK = 4
QUADS = 4
N, T, D, DV, NQ = 1024, 4096, 1024, 256, 256
PAGE = 512
CAP = 2.0
PAGES = N // PAGE
POOL_PAGES = T // PAGE
PASSES = D // PAGE
QT = NQ // P
KIB = 1024
FLOPS = 2 * NQ * N * (D + DV)
BYTES = 4 * D * NQ + 4 * P * T + 2 * 16 * T + 4 * P * DV * POOL_PAGES + 16 * DV * POOL_PAGES + 4 * T + 8 * NQ * DV


def tile_attend_pkv4_gate_cap_kernel(
    tc, qT, k_words, k_scales, v_words, v_scales, vs, og, offs, voffs, out
):
    nc = tc.nc
    with ExitStack() as ctx:
        lists = ctx.enter_context(tc.tile_pool(name="lists", bufs=1))
        sb = ctx.enter_context(tc.tile_pool(name="sb", bufs=1))
        arena = ctx.enter_context(tc.tile_pool(name="arena", bufs=1))
        ps = ctx.enter_context(tc.psum_pool(name="ps", bufs=1))

        def sbt(name, shape, dtype):
            return sb.tile(shape, dtype, name=name, align_bytes=64)

        def placed(name, shape, dtype, kib):
            return arena.tile(shape, dtype, name=name, offset=kib * KIB, align_bytes=64)

        def bank(name, tag, shape):
            return ps.tile(shape, F32, name=name, tag=tag)

        def zero_odd(words):
            cut = words.shape[1] // 2 - 1
            nc.vector.memset(words[:, :cut], 0)
            nc.vector.memset(words[:, cut:], 0)

        offs_sb = lists.tile([P, N // 16], U16, name="offs_sb")
        voffs_sb = lists.tile([P, PAGES * DV // 16], U16, name="voffs_sb")

        ks_pool = placed("ks_pool", [P, T], U8, 12)
        ks_words = ks_pool[:].bitcast(I32)
        vs_pool = sbt("vs_pool", [P, T], F32)
        kw_pool = sbt("kw_pool", [P, T], I32)
        nc.sync.dma_start(ks_words[32:64, :], k_scales.rearrange("o r t -> r o t").bitcast(I32))
        nc.sync.dma_start(offs_sb[:], offs)
        nc.sync.dma_start(vs_pool[P - 1:P, :], vs[0:1, :])
        nc.sync.dma_start(kw_pool[:], k_words[0].rearrange("p t b -> p (t b)").bitcast(I32))

        zero_odd(ks_words[0:32, :])
        zero_odd(ks_words[64:P, :])
        nc.gpsimd.memset(vs_pool[0:P - 1, :], 0.0)
        vsc_pool = sbt("vsc_pool", [P, POOL_PAGES * DV], U8)
        nc.gpsimd.memset(vsc_pool[:].bitcast(I32)[0:112, :], 0)
        ident = sbt("ident", [P, P], F32)
        nc.gpsimd.memset(ident[:], 0.0)
        nc.gpsimd.affine_select(
            out=ident[:], in_=ident[:], pattern=[[-1, P]], compare_op=ALU.not_equal,
            fill=1.0, base=0, channel_multiplier=1,
        )
        ks_plane = [placed("ks_plane%d" % g, [P, PASSES * PAGE], U8, 12 + g) for g in range(PAGES)]
        vsc_plane = placed("vsc_plane", [P, PAGES * DV], U8, 14)

        ks_g = sbt("ks_g", [P, N], U8)
        nc.vector.tensor_copy(ks_g[:], ks_pool[:].indirect(offs_sb[:]))
        vs_g = sbt("vs_g", [P, N], F32)
        nc.vector.tensor_copy(vs_g[:], vs_pool[:].indirect(offs_sb[:]))

        q_rows = qT[0].rearrange("(o p j) w -> o p j w", o=PASSES, j=PACK)
        q_raw = [placed("q_raw%d" % o, [P, PACK, NQ], F32, 4 * o) for o in range(PASSES)]

        def move_key_planes(g, queue):
            for q in (0, 2, 1, 3):
                queue.dma_start(
                    ks_plane[g][:].bitcast(I32)[32 * q:32 * q + PACK, :],
                    ks_g[:, g * PAGE:(g + 1) * PAGE].bitcast(I32)[32 + 8 * q:32 + 8 * (q + 1), :],
                )

        nc.sync.dma_start(q_raw[0][:], q_rows[0])
        move_key_planes(0, nc.scalar)
        nc.sync.dma_start(q_raw[1][:], q_rows[1])
        nc.sync.dma_start(voffs_sb[:], voffs)
        nc.sync.dma_start(
            vsc_pool[:].bitcast(I32)[112:P, :].rearrange("f (u e) -> f u e", u=POOL_PAGES),
            v_scales.rearrange("u f e -> f u e").bitcast(I32),
        )
        move_key_planes(1, nc.sync)
        vw_pool = sbt("vw_pool", [P, POOL_PAGES * DV], I32)
        nc.sync.dma_start(
            vw_pool[:].rearrange("p (u e) -> p u e", u=POOL_PAGES),
            v_words.rearrange("u p e b -> p u (e b)").bitcast(I32),
        )
        vs_col = [sbt("vs_col%d" % g, [P, PACK], F32) for g in range(PAGES)]
        for g in (1, 0):
            nc.sync.dma_start(vs_col[g][:], vs_g[P - 1:P, g * PAGE:(g + 1) * PAGE])
        og_sb = sbt("og_sb", [P, QT, DV], F32)
        nc.sync.dma_start(og_sb[:], og[0].rearrange("(h p) e -> p h e", p=P))

        q_bf = [sbt("q_bf%d" % h, [P, PASSES, P * PACK], BF16) for h in range(QT)]
        for o in range(PASSES):
            for h in range(QT):
                nc.scalar.activation(
                    out=q_bf[h][:, o, :].rearrange("p (c i t) -> p c t i", i=4, t=PACK),
                    in_=q_raw[o][:, :, h * P:(h + 1) * P].rearrange("p t (c i) -> p c t i", i=4), func=ACT.Copy,
                )
        q_codes = [sbt("q_codes%d" % h, [P, PASSES * P], U32) for h in range(QT)]
        q_scales = [sbt("q_scales%d" % h, [P, PASSES * P], U8) for h in range(QT)]
        k_g = [sbt("k_g%d" % g, [P, PAGE], U32) for g in range(PAGES)]
        k_parted = [sbt("k_parted0", [P, PASSES * PAGE * 2], U8), placed("k_parted1", [P, PASSES * PAGE * 2], U8, 0)]

        def gather_keys(g):
            cols = slice(g * PAGE // 16, (g + 1) * PAGE // 16)
            nc.vector.tensor_copy(k_g[g][:], kw_pool[:].bitcast(U32).indirect(offs_sb[:, cols]))

        def part_keys(g):
            nc.vector.tensor_copy(
                k_parted[g][:].bitcast(U16).rearrange("p (o a n) -> p a o n", o=PASSES, a=2),
                k_g[g][:].bitcast(U16).rearrange("p (a n o) -> p a o n", o=PASSES, a=2),
            )

        def quantize_q(h, passes):
            cols = slice(passes.start * P, passes.stop * P)
            nc.vector.quantize_mx(
                out=q_codes[h][:, cols].bitcast(FP8X4), scales=q_scales[h][:, cols],
                in_=q_bf[h][:, passes, :].rearrange("p o c -> p (o c)"),
            )

        gather_keys(0)
        gather_keys(1)
        part_keys(0)
        for h in range(QT):
            quantize_q(h, slice(0, 1))
        part_keys(1)
        for h in range(QT):
            quantize_q(h, slice(1, PASSES))

        vsc_g = placed("vsc_g", [P, PAGES * DV], U8, 6)
        nc.vector.tensor_copy(vsc_g[:], vsc_pool[:].indirect(voffs_sb[:]))
        for q in range(QUADS):
            nc.sync.dma_start(
                vsc_plane[:].bitcast(I32)[32 * q:32 * q + PACK, :],
                vsc_g[:].bitcast(I32)[112 + PACK * q:112 + PACK * (q + 1), :],
            )

        half = [sbt("half%d" % h, [P, N], F32) for h in range(QT)]
        acc = [[bank("score%d%d" % (h, g), "s%d" % (2 * h + g), [P, PAGE]) for g in range(PAGES)] for h in range(QT)]

        def score_pass(h, g, o):
            nc.tensor.matmul_mx(
                out=acc[h][g][:],
                lhsT=q_codes[h][:, o * P:(o + 1) * P].bitcast(FP8X4),
                lhsT_scale=q_scales[h][:, o * P:(o + 1) * P],
                rhs=k_parted[g][:, o * 2 * PAGE:(o + 1) * 2 * PAGE].bitcast(FP4X4),
                rhs_scale=ks_plane[g][:, o * PAGE:(o + 1) * PAGE],
                start=(o == 0), stop=(o == PASSES - 1),
            )
            if o == PASSES - 1:
                nc.scalar.activation(
                    out=half[h][:, g * PAGE:(g + 1) * PAGE].rearrange("p (r s) -> p r s", r=PACK),
                    in_=acc[h][g][:].rearrange("p (s r) -> p r s", r=PACK),
                    func=ACT.Tanh, scale=1.0 / CAP,
                )

        for o in range(PASSES):
            for h in range(QT):
                score_pass(h, 0, o)
        for h in range(QT):
            for o in range(PASSES):
                score_pass(h, 1, o)

        neg_c = [[placed("neg_c%d%d" % (h, g), [P, PAGE], F32, 20 + 4 * h + 2 * g) for g in range(PAGES)] for h in range(QT)]
        neg_m = [[sbt("neg_m%d%d" % (h, g), [P, 1], F32) for g in range(PAGES)] for h in range(QT)]
        prob = [[placed("prob%d%d" % (h, g), [P, PAGE], F32, 0 if h + g == 0 else 28 + 4 * h + 2 * g) for g in range(PAGES)] for h in range(QT)]
        part_sum = sbt("part_sum", [P, PAGES, QT], F32)
        first_sum = sbt("first_sum", [P, 2], F32)
        row_sum = sbt("row_sum", [P, QT], F32)
        for g in range(PAGES):
            for h in range(QT):
                nc.vector.tensor_scalar(
                    out=neg_c[h][g][:], in0=half[h][:, g * PAGE:(g + 1) * PAGE], scalar1=-CAP,
                    scalar2=neg_m[h][0][:] if g else None,
                    op0=ALU.mult, op1=ALU.min, accum_out=neg_m[h][g][:],
                )

        def weights(h, g, cols, total):
            nc.scalar.activation(
                out=prob[h][g][:, cols], in_=neg_c[h][g][:, cols], func=ACT.Exp,
                bias=neg_m[h][PAGES - 1][:], scale=-1.0, accum_out=total,
            )

        for a in range(2):
            weights(0, 0, slice(a * PAGE // 2, (a + 1) * PAGE // 2), first_sum[:, a:a + 1])
        for h, g in ((0, 1), (1, 0), (1, 1)):
            weights(h, g, slice(0, PAGE), part_sum[:, g, h:h + 1])
        joined = sbt("joined", [P, 1], F32)
        nc.scalar.activation(out=joined[:], in_=first_sum[:, 0:1], func=ACT.Identity, bias=first_sum[:, 1:2])
        for h, page0 in ((1, part_sum[:, 0, 1:2]), (0, joined[:])):
            nc.scalar.activation(out=row_sum[:, h:h + 1], in_=page0, func=ACT.Identity, bias=part_sum[:, 1, h:h + 1])

        v_g = sbt("v_g", [P, PAGES * DV], U32)
        nc.vector.tensor_copy(v_g[:], vw_pool[:].bitcast(U32).indirect(voffs_sb[:]))

        gate_t = placed("gate_t", [P, QT, DV], F32, 26)
        gate = sbt("gate", [P, QT, DV], F32)
        nc.scalar.activation(out=gate_t[:], in_=og_sb[:], func=ACT.Tanh, scale=0.5)
        nc.scalar.activation(out=gate[:], in_=gate_t[:], func=ACT.Copy, scale=0.5, bias=0.5)

        w_bf = [sbt("w_bf%d" % h, [P, PAGES, P, PACK], BF16) for h in range(QT)]
        w_codes = [placed("w_codes%d" % h, [P, PAGES * P], U32, 32 + 2 * h) for h in range(QT)]
        w_scales = [sbt("w_scales%d" % h, [P, PAGES * P], U8) for h in range(QT)]

        def weigh(h, g):
            p_t = bank("p_t%d%d" % (h, g), "t%d" % (2 * h + g), [P, PACK, P])
            for r in range(PACK):
                nc.tensor.transpose(p_t[:, r, :], prob[h][g][:, r * P:(r + 1) * P], ident[:])
            nc.vector.tensor_tensor(
                out=w_bf[h][:, g].rearrange("p (c e) r -> p c r e", e=2),
                in0=p_t[:].rearrange("p r (c e) -> p c r e", e=2),
                in1=vs_col[g][:].unsqueeze(1).unsqueeze(3).to_broadcast([P, P // 2, PACK, 2]), op=ALU.mult,
            )

        def quantize_w(h, pages):
            cols = slice(pages.start * P, pages.stop * P)
            nc.vector.quantize_mx(
                out=w_codes[h][:, cols].bitcast(FP8X4), scales=w_scales[h][:, cols],
                in_=w_bf[h][:, pages].rearrange("p g q r -> p (g q r)"),
            )

        pieces = [(0, 0, DV), (1, 0, DV // 2), (1, DV // 2, DV)]
        y = [bank("y%d" % i, "s%d" % i, [P, hi - lo]) for i, (h, lo, hi) in enumerate(pieces)]

        def value_pass(i, g):
            h, lo, hi = pieces[i]
            cols = slice(g * DV + lo, g * DV + hi)
            nc.tensor.matmul_mx(
                out=y[i][:],
                lhsT=w_codes[h][:, g * P:(g + 1) * P].bitcast(FP8X4), lhsT_scale=w_scales[h][:, g * P:(g + 1) * P],
                rhs=v_g[:, cols].bitcast(FP8X4), rhs_scale=vsc_plane[:, cols],
                start=(g == 0), stop=(g == PAGES - 1),
            )

        inv_sum = sbt("inv_sum", [P, QT], F32)

        def finish(i):
            h, lo, hi = pieces[i]
            res = sbt("res%d" % i, [P, hi - lo], F32)
            nc.vector.scalar_tensor_tensor(
                out=res[:], in0=y[i][:], scalar=inv_sum[:, h:h + 1], in1=gate[:, h, lo:hi],
                op0=ALU.mult, op1=ALU.mult,
            )
            nc.sync.dma_start(out[0, h * P:(h + 1) * P, lo:hi], res[:])

        weigh(0, 0)
        weigh(0, 1)
        weigh(1, 0)
        quantize_w(0, slice(0, PAGES))
        weigh(1, 1)
        value_pass(0, 0)
        value_pass(0, 1)
        quantize_w(1, slice(0, 1))
        nc.vector.reciprocal(inv_sum[:], row_sum[:])
        quantize_w(1, slice(1, PAGES))
        for g in range(PAGES):
            value_pass(1, g)
            value_pass(2, g)
        for i in range(len(pieces)):
            finish(i)
